import numpy as np
import ml_dtypes


def mxq(x, axis, fmt="e4m3"):
    dtype, down = {"e4m3": (ml_dtypes.float8_e4m3fn, 7), "e5m2": (ml_dtypes.float8_e5m2, 14)}[fmt]
    v = np.moveaxis(np.asarray(x, np.float32).astype(ml_dtypes.bfloat16).astype(np.float64), axis, -1)
    blocks = v.reshape(v.shape[:-1] + (-1, 32))
    amax = np.abs(blocks).max(-1, keepdims=True)
    byte = np.maximum(np.where(amax > 0, np.frexp(amax)[1] - 1 + 127, 0) - down, 1)
    scale = np.exp2(byte - 127.0)
    codes = (blocks / scale).astype(np.float32).astype(dtype).astype(np.float64)
    return np.moveaxis((codes * scale).reshape(v.shape), -1, axis)


WIDE = False


def mx_kscale(k):
    if not WIDE:
        return np.ones(k)
    levels = np.array([10, -10, 5, -5, 0])
    if k % 512:
        return np.exp2(np.random.permutation(np.resize(levels, k // 32))).repeat(32)
    a = np.empty((k // 512, 16))
    for p in range(k // 512):
        a[p, :8] = np.random.permutation(np.resize(levels, 8))
        for g in range(8):
            far = levels[np.abs(levels - a[p, g]) >= 10]
            a[p, g + 8] = far[np.random.randint(len(far))]
    return np.exp2(a.ravel()).repeat(32)


def f64(x):
    return np.asarray(x).astype(np.float64)


def striped(idx):
    return np.tile(idx.reshape(-1, 16).T, (8, 1)).astype(np.uint16)


def unstriped(offs):
    return offs[:16].T.reshape(-1).astype(np.int64)


E2M1 = np.array([0.0, 0.5, 1.0, 1.5, 2.0, 3.0, 4.0, 6.0, -0.0, -0.5, -1.0, -1.5, -2.0, -3.0, -4.0, -6.0])


def pack_weight(w, fmt):
    k, n = w.shape
    w = f64(np.asarray(w, np.float32).astype(ml_dtypes.bfloat16)).reshape(k // 32, 32, n)
    amax = np.abs(w).max(1)
    if fmt == "e4m3":
        byte = np.frexp(amax)[1] - 1 + 127 - 7
    else:
        mant, ex = np.frexp(amax / 6.0)
        byte = np.where(mant > 0.5, ex, ex - 1) + 127
    byte = np.clip(np.where(amax > 0, byte, 1), 1, 254)
    scaled = (w * np.exp2(127.0 - byte)[:, None, :]).reshape(k, n).astype(np.float32)
    by_word = np.ascontiguousarray(scaled.reshape(k // 512, 128, 4, n).transpose(0, 1, 3, 2))
    if fmt == "e4m3":
        words = by_word.astype(ml_dtypes.float8_e4m3fn).view(np.uint8)
    else:
        c = by_word.astype(ml_dtypes.float4_e2m1fn).view(np.uint8) & 0xF
        words = (c[..., 0::2] | (c[..., 1::2] << 4)).reshape(k // 512, 128, 2 * n)
    return np.ascontiguousarray(words), np.ascontiguousarray(byte.astype(np.uint8).reshape(k // 512, 16, n))


def unpack_weight(words, scales, fmt):
    g, _, n = scales.shape
    words = np.ascontiguousarray(words).reshape(g, 128, n, -1)
    if fmt == "e4m3":
        vals = words.view(ml_dtypes.float8_e4m3fn).astype(np.float64)
    else:
        nib = np.empty((g, 128, n, 4), np.uint8)
        nib[..., 0::2] = words & 0xF
        nib[..., 1::2] = words >> 4
        vals = E2M1[nib]
    vals = vals * np.repeat(np.exp2(scales.astype(np.float64) - 127.0), 8, axis=1)[..., None]
    return vals.transpose(0, 1, 3, 2).reshape(g * 512, n)


def gelu(v):
    return 0.5 * v * (1.0 + np.tanh(np.sqrt(2.0 / np.pi) * (v + 0.044715 * v**3)))


K, T, E, C, H, TOP, COPIES = 512, 512, 6, 128, 512, 3, 384
PAD = 64


def by_expert(wq, xq):
    return np.concatenate([wq[e].T @ xq[:, e * C:(e + 1) * C] for e in range(E)], axis=1)


def setup_inputs():
    n = np.random.standard_normal
    s = mx_kscale(K)
    u = mx_kscale(H)
    left = TOP * T - E * C - COPIES
    deal = np.repeat(np.arange(E + 2), [C] * E + [COPIES, left]).reshape(TOP, T)[:, np.random.permutation(T)]
    deal = np.take_along_axis(deal, np.argsort(np.random.rand(TOP, T), axis=0), axis=0)
    for _ in range(8):
        s_, t_ = np.random.permutation(T).reshape(2, -1); r = np.random.randint(TOP, size=T // 2); x, y = deal[r, s_].copy(), deal[r, t_].copy()
        ok = ~((deal[:, s_] == y).any(0) | (deal[:, t_] == x).any(0)); deal[r[ok], s_[ok]] = y[ok]; deal[r[ok], t_[ok]] = x[ok]
    order = np.lexsort((np.random.rand(TOP * T), deal.reshape(-1)))[:E * C]
    slot_token = order % T
    pos = np.where(deal == E, E * C + np.arange(T), E * C + T + np.arange(T) % PAD).reshape(-1); pos[order] = np.arange(E * C); pos = pos.reshape(TOP, T)
    g = np.random.uniform(0.5, 1.5, (TOP, T)); g = g / g.sum(0)
    xf = n((K, T))
    x = pack_weight(xf * s[:, None], "e4m3")
    return {
        "x_words": x[0],
        "x_scales": x[1],
        "xr": (xf).astype(np.float32),
        "w1": (n((E, K, H)) / np.sqrt(K) / s[None, :, None]).astype(np.float32),
        "w3": (n((E, K, H)) / np.sqrt(K) / s[None, :, None] * u).astype(np.float32),
        "w2": (n((E, H, K)) / np.sqrt(H) / u[None, :, None]).astype(np.float32),
        "gate": np.stack([np.tile(r, (128, 1)) for r in g]).astype(np.float32),
        "offs": striped(slot_token),
        "pos1": striped(pos[0]),
        "pos2": striped(pos[1]),
        "pos3": striped(pos[2]),
    }


def reference(x_words, x_scales, xr, w1, w3, w2, gate, offs, pos1, pos2, pos3):
    w1q = mxq(f64(w1), 1, "e4m3")
    w3q = mxq(f64(w3), 1, "e4m3")
    w2q = mxq(f64(w2), 1, "e4m3")
    idx = unstriped(offs)
    xq = unpack_weight(x_words, x_scales, "e4m3")[:, idx]
    h = gelu(by_expert(w1q, xq)) * by_expert(w3q, xq)
    y = by_expert(w2q, mxq(h, 0, "e4m3"))
    y = np.concatenate([y, f64(xr), np.zeros((K, PAD))], axis=1)
    out = sum(f64(gate[r, :1]) * y[:, unstriped(p)] for r, p in enumerate((pos1, pos2, pos3)))
    return out

@@ -1,0 +1,219 @@
+from contextlib import ExitStack
+
+import concourse.mybir as mybir
+from concourse.masks import make_identity
+
+K, T, E, C, H, TOP, PAD = 512, 512, 6, 128, 512, 3, 64
+SLOTS = E * C
+WIN = SLOTS + T + PAD
+FLOPS = 2 * 3 * SLOTS * K * H
+
+F32 = mybir.dt.float32
+BF16 = mybir.dt.bfloat16
+I32 = mybir.dt.int32
+U32 = mybir.dt.uint32
+U16 = mybir.dt.uint16
+U8 = mybir.dt.uint8
+FP8X4 = mybir.dt.float8_e4m3fn_x4
+MULT = mybir.AluOpType.mult
+ADD = mybir.AluOpType.add
+GELU = mybir.ActivationFunctionType.Gelu_apprx_tanh
+
+P = 128
+PACK = 4
+BLOCKS = K // P
+PAIR = 2 * C
+VEC_COLS = 256
+LAST_VEC_COLS = 344
+
+
+def tile_moe_cpy_glu_gelu_kernel(tc, x_words, x_scales, xr, w1, w3, w2, gate, offs, pos1, pos2, pos3, out):
+    nc = tc.nc
+    with ExitStack() as ctx:
+        keep = ctx.enter_context(tc.tile_pool(name="keep", bufs=1))
+        ring3 = ctx.enter_context(tc.tile_pool(name="ring3", bufs=3))
+        ring2 = ctx.enter_context(tc.tile_pool(name="ring2", bufs=2))
+        acc = ctx.enter_context(tc.psum_pool(name="acc", bufs=6))
+        turn = ctx.enter_context(tc.psum_pool(name="turn", bufs=2))
+
+        offs_sb = keep.tile([P, SLOTS // 16], U16, name="offs_sb")
+        nc.sync.dma_start(offs_sb[:], offs)
+        tok_words = keep.tile([P, T], U32, name="tok_words", align_bytes=64)
+        nc.sync.dma_start(tok_words[:].bitcast(I32), x_words[0].rearrange("p t d -> p (t d)").bitcast(I32))
+        tok_scales = keep.tile([P, T], U8, name="tok_scales", align_bytes=64)
+        nc.gpsimd.memset(tok_scales[:].bitcast(I32), 0)
+        for q in range(4):
+            nc.sync.dma_start(tok_scales[32 * q : 32 * q + 4, :].bitcast(I32), x_scales[0, 4 * q : 4 * q + 4, :].bitcast(I32))
+        gate_cols = keep.tile([P, TOP, 4], F32, name="gate_cols")
+        nc.scalar.dma_start(gate_cols[:], gate[:, 0, :].rearrange("r (p c) -> p r c", c=4))
+        warm = keep.tile([P, 16], F32, name="warm")
+        nc.vector.memset(warm[:, :8], 0.0)
+        nc.scalar.activation(warm[:, 8:], warm[:, :8], GELU)
+
+        raw13 = {}
+        pos_sb = []
+        for e in range(E):
+            for m, w in enumerate((w1, w3)):
+                raw13[e, m] = keep.tile([P, PACK, H], F32, name=f"raw13_{e}_{m}", align_bytes=64)
+                nc.sync.dma_start(raw13[e, m][:], w[e].rearrange("(p j) c -> p j c", j=PACK))
+            if e == 0:
+                for r, pos in enumerate((pos1, pos2, pos3)):
+                    pos_sb.append(keep.tile([P, T // 16], U16, name=f"pos_sb{r}"))
+                    nc.sync.dma_start(pos_sb[r][:], pos)
+        raw2 = []
+        window = []
+        for b in range(BLOCKS):
+            raw2.append(keep.tile([P, E, PACK, P], F32, name=f"raw2_{b}", align_bytes=64))
+            for e in range(E):
+                nc.sync.dma_start(raw2[b][:, e, :, :], w2[e].rearrange("(p j) n -> p j n", j=PACK)[:, :, b * P : (b + 1) * P])
+            window.append(keep.tile([P, WIN], F32, name=f"window{b}"))
+            nc.sync.dma_start(window[b][:, SLOTS : SLOTS + T], xr[b * P : (b + 1) * P, :])
+            nc.gpsimd.memset(window[b][:, SLOTS + T :], 0.0)
+
+        ident = keep.tile([P, P], F32, name="ident")
+        make_identity(nc, ident[:])
+
+        slot_words = keep.tile([P, SLOTS], U32, name="slot_words", align_bytes=64)
+        slot_scales = keep.tile([P, SLOTS], U8, name="slot_scales", align_bytes=64)
+        half = SLOTS // 2
+        for a in range(2):
+            part = offs_sb[:, a * half // 16 : (a + 1) * half // 16]
+            nc.vector.tensor_copy(slot_words[:, a * half : (a + 1) * half], tok_words[:].indirect(part))
+            nc.vector.tensor_copy(slot_scales[:, a * half : (a + 1) * half], tok_scales[:].indirect(part))
+
+        gates = keep.tile([P, TOP, T], F32, name="gates")
+        for r in range(TOP):
+            spread = acc.tile([P, 4, P], F32, name="spread", tag="acc")
+            for c in range(4):
+                nc.tensor.transpose(spread[:, c, :], gate_cols[:, r, c : c + 1].to_broadcast([P, P]), ident[:])
+            nc.scalar.copy(gates[:, r, :].rearrange("p (n c) -> p n c", c=4), spread[:].rearrange("p c n -> p n c"))
+
+        def interleave(copy, grouped, raw):
+            copy(grouped.rearrange("p (c i) j -> p c j i", i=4), raw.rearrange("p j (c i) -> p c j i", i=4))
+
+        h_words = keep.tile([P, SLOTS], U32, name="h_words", align_bytes=64)
+        h_scales = keep.tile([P, SLOTS], U8, name="h_scales", align_bytes=64)
+
+        stage = [keep.tile([P, H * PACK], BF16, name=f"stage{i}", align_bytes=64) for i in range(2)]
+        stage_b = [keep.tile([P, PAIR * PACK], BF16, name=f"stage_b{i}", align_bytes=64) for i in range(2)]
+        sums = {}
+        turned = {}
+
+        def cast13(e, m):
+            cut = LAST_VEC_COLS if (e, m) == (E - 1, 1) else VEC_COLS
+            grouped = stage[m][:].rearrange("p (c j) -> p c j", j=PACK)
+            interleave(nc.vector.tensor_copy, grouped[:, :cut, :], raw13[e, m][:, :, :cut])
+            interleave(nc.scalar.copy, grouped[:, cut:, :], raw13[e, m][:, :, cut:])
+
+        def product13(e, m):
+            slots = slice(e * C, (e + 1) * C)
+            w_words = ring3.tile([P, H], U32, name="w_words", align_bytes=64)
+            w_scales = ring3.tile([P, H], U8, name="w_scales", align_bytes=64)
+            nc.vector.quantize_mx(out=w_words[:].bitcast(FP8X4), scales=w_scales[:], in_=stage[m][:])
+            sums[e, m] = acc.tile([P, H], F32, name="sums", tag="acc")
+            nc.tensor.matmul_mx(out=sums[e, m][:], lhsT=slot_words[:, slots].bitcast(FP8X4), lhsT_scale=slot_scales[:, slots],
+                                rhs=w_words[:].bitcast(FP8X4), rhs_scale=w_scales[:], start=True, stop=True)
+
+        def hidden_rows(e, pairs):
+            nc.vector.tensor_tensor(pairs.bitcast(BF16), sums[e, 1][:], raw13[e, 1][:, PACK - 1, :], MULT)
+            turned[e] = turn.tile([P, 2, C], F32, name="turned")
+            for u in range(2):
+                nc.tensor.transpose(turned[e][:, u, :], pairs[:, u : H // 2 : 2], ident[:])
+
+        def hidden_codes(e, pairs):
+            slots = slice(e * C, (e + 1) * C)
+            nc.scalar.copy(pairs.rearrange("p (s u) -> p s u", u=2), turned[e][:].rearrange("p u s -> p s u"))
+            nc.vector.quantize_mx(out=h_words[:, slots].bitcast(FP8X4), scales=h_scales[:, slots], in_=pairs.bitcast(BF16))
+
+        for e in range(E):
+            cast13(e, 0)
+            if e > 0:
+                hidden_rows(e - 1, raw13[e, 0][:, 0, : H // 2])
+            product13(e, 0)
+            cast13(e, 1)
+            nc.scalar.activation(raw13[e, 1][:, PACK - 1, :], sums[e, 0][:], GELU)
+            product13(e, 1)
+            if e > 0:
+                hidden_codes(e - 1, raw13[e, 1][:, PACK - 2, H // 2 :])
+
+        codes2 = {}
+
+        def cast2(b, e):
+            flat, u = (stage[b % 2], e) if e < 4 else (stage_b[b % 2], e - 4)
+            grouped = flat[:].rearrange("p (c j) -> p c j", j=PACK)
+            copy = nc.vector.tensor_copy if (b == 0 and e in (0, 1, 5)) else nc.scalar.copy
+            interleave(copy, grouped[:, u * P : (u + 1) * P, :], raw2[b][:, e, :, :])
+
+        def product2(b, experts):
+            w2_words, w2_scales, banks = codes2[b]
+            cols = slice(experts[0] * P, (experts[-1] + 1) * P)
+            flat = stage[b % 2] if experts[0] == 0 else stage_b[b % 2]
+            nc.vector.quantize_mx(out=w2_words[:, cols].bitcast(FP8X4), scales=w2_scales[:, cols], in_=flat[:])
+            for e in experts:
+                slots = slice(e * C, (e + 1) * C)
+                nc.tensor.matmul_mx(out=banks[e % 2][:, e // 2, :], lhsT=w2_words[:, slots].bitcast(FP8X4), lhsT_scale=w2_scales[:, slots],
+                                    rhs=h_words[:, slots].bitcast(FP8X4), rhs_scale=h_scales[:, slots], start=True, stop=True)
+
+        def open_block(b):
+            w2_words = ring2.tile([P, SLOTS], U32, name="w2_words", align_bytes=64)
+            w2_scales = ring2.tile([P, SLOTS], U8, name="w2_scales", align_bytes=64)
+            banks = [acc.tile([P, E // 2, C], F32, name=f"y_sums{i}", tag="acc") for i in range(2)]
+            codes2[b] = (w2_words, w2_scales, banks)
+
+        def close_block(b):
+            by_pair = window[b][:, :SLOTS].rearrange("p (a u s) -> p a u s", u=2, s=C)
+            for u in range(2):
+                copy = nc.vector.tensor_copy if (b, u) == (0, 1) else nc.scalar.copy
+                copy(by_pair[:, :, u, :], codes2[b][2][u][:])
+
+        def first_four(b):
+            open_block(b)
+            for e in range(4):
+                cast2(b, e)
+            product2(b, range(4))
+
+        def last_two(b):
+            for e in range(4, E):
+                cast2(b, e)
+            product2(b, range(4, E))
+            close_block(b)
+
+        def spent(e):
+            return raw2[0][:, e, 0:2, :].rearrange("p j n -> p (j n)")
+
+        open_block(0)
+        cast2(0, 0)
+        cast2(0, 1)
+        hidden_rows(E - 1, spent(1))
+        cast2(0, 2)
+        cast2(0, 3)
+        product2(0, range(4))
+        cast2(0, 4)
+        hidden_codes(E - 1, spent(4))
+        cast2(0, 5)
+        product2(0, range(4, E))
+        close_block(0)
+        for b in range(BLOCKS):
+            more = b + 1 < BLOCKS
+            spare = (b + 1) % 2
+            picked0 = ring2.tile([P, T], F32, name="picked0")
+            picked1 = ring2.tile([P, T], F32, name="picked1")
+            picked2 = stage[spare][:, : 2 * T].bitcast(F32)
+            two = stage_b[spare][:].bitcast(F32)
+            nc.vector.tensor_tensor(picked0[:], window[b][:].indirect(pos_sb[0][:]), gates[:, 0, :], MULT)
+            nc.vector.tensor_tensor(picked1[:], window[b][:].indirect(pos_sb[1][:]), gates[:, 1, :], MULT)
+            if more:
+                first_four(b + 1)
+            nc.vector.tensor_tensor(picked2, window[b][:].indirect(pos_sb[2][:]), gates[:, 2, :], MULT)
+            if more:
+                last_two(b + 1)
+            total = ring2.tile([P, T], F32, name="total")
+            halves = (slice(0, T // 2), slice(T // 2, T))
+            for cols in halves:
+                nc.vector.tensor_tensor(two[:, cols], picked0[:, cols], picked1[:, cols], ADD)
+            for cols in halves:
+                nc.vector.tensor_tensor(total[:, cols], two[:, cols], picked2[:, cols], ADD)
+                if not more:
+                    nc.sync.dma_start(out[b * P : (b + 1) * P, cols], total[:, cols])
+            if more:
+                nc.sync.dma_start(out[b * P : (b + 1) * P, :], total[:])

@@ -24,7 +24,6 @@ PACK = 4
 BLOCKS = K // P
 PAIR = 2 * C
 VEC_COLS = 256
-LAST_VEC_COLS = 344
 
 
 def tile_moe_cpy_glu_gelu_kernel(tc, x_words, x_scales, xr, w1, w3, w2, gate, offs, pos1, pos2, pos3, out):
@@ -51,22 +50,31 @@ def tile_moe_cpy_glu_gelu_kernel(tc, x_words, x_scales, xr, w1, w3, w2, gate, of
         nc.scalar.activation(warm[:, 8:], warm[:, :8], GELU)
 
         raw13 = {}
+        last_halves = []
         pos_sb = []
         for e in range(E):
             for m, w in enumerate((w1, w3)):
-                raw13[e, m] = keep.tile([P, PACK, H], F32, name=f"raw13_{e}_{m}", align_bytes=64)
-                nc.sync.dma_start(raw13[e, m][:], w[e].rearrange("(p j) c -> p j c", j=PACK))
+                rows = w[e].rearrange("(p j) c -> p j c", j=PACK)
+                if (e, m) == (E - 1, 1):
+                    for a in range(2):
+                        last_halves.append(keep.tile([P, PACK, H // 2], F32, name=f"last_half{a}", align_bytes=64))
+                        nc.sync.dma_start(last_halves[a][:], rows[:, :, a * H // 2 : (a + 1) * H // 2])
+                else:
+                    raw13[e, m] = keep.tile([P, PACK, H], F32, name=f"raw13_{e}_{m}", align_bytes=64)
+                    nc.sync.dma_start(raw13[e, m][:], rows)
             if e == 0:
                 for r, pos in enumerate((pos1, pos2, pos3)):
                     pos_sb.append(keep.tile([P, T // 16], U16, name=f"pos_sb{r}"))
                     nc.sync.dma_start(pos_sb[r][:], pos)
-        raw2 = []
+        raw2 = {}
         window = []
         for b in range(BLOCKS):
-            raw2.append(keep.tile([P, E, PACK, P], F32, name=f"raw2_{b}", align_bytes=64))
+            window.append(keep.tile([P, WIN], F32, name=f"window{b}", align_bytes=64))
+            landing = keep.tile([P, E, PACK, P], F32, name=f"landing{b}", align_bytes=64)
             for e in range(E):
-                nc.sync.dma_start(raw2[b][:, e, :, :], w2[e].rearrange("(p j) n -> p j n", j=PACK)[:, :, b * P : (b + 1) * P])
-            window.append(keep.tile([P, WIN], F32, name=f"window{b}"))
+                lodger = e == (4 if b == 0 else 5)
+                raw2[b, e] = window[b][:, : 4 * C].rearrange("p (j n) -> p j n", j=PACK) if lodger else landing[:, e, :, :]
+                nc.sync.dma_start(raw2[b, e], w2[e].rearrange("(p j) n -> p j n", j=PACK)[:, :, b * P : (b + 1) * P])
             nc.sync.dma_start(window[b][:, SLOTS : SLOTS + T], xr[b * P : (b + 1) * P, :])
             nc.gpsimd.memset(window[b][:, SLOTS + T :], 0.0)
 
@@ -95,27 +103,40 @@ def tile_moe_cpy_glu_gelu_kernel(tc, x_words, x_scales, xr, w1, w3, w2, gate, of
         h_scales = keep.tile([P, SLOTS], U8, name="h_scales", align_bytes=64)
 
         stage = [keep.tile([P, H * PACK], BF16, name=f"stage{i}", align_bytes=64) for i in range(2)]
-        stage_b = [keep.tile([P, PAIR * PACK], BF16, name=f"stage_b{i}", align_bytes=64) for i in range(2)]
+        wide = [keep.tile([P, 4 * T], BF16, name=f"wide{i}", align_bytes=64) for i in range(2)]
+        stage_b = [wide[i][:, T : 3 * T] for i in range(2)]
         sums = {}
         turned = {}
 
+        acts = {}
+
         def cast13(e, m):
-            cut = LAST_VEC_COLS if (e, m) == (E - 1, 1) else VEC_COLS
             grouped = stage[m][:].rearrange("p (c j) -> p c j", j=PACK)
-            interleave(nc.vector.tensor_copy, grouped[:, :cut, :], raw13[e, m][:, :, :cut])
-            interleave(nc.scalar.copy, grouped[:, cut:, :], raw13[e, m][:, :, cut:])
+            if (e, m) == (E - 1, 1):
+                interleave(nc.scalar.copy, grouped[:, : H // 2, :], last_halves[0][:])
+                interleave(nc.vector.tensor_copy, grouped[:, H // 2 :, :], last_halves[1][:])
+            else:
+                interleave(nc.vector.tensor_copy, grouped[:, :VEC_COLS, :], raw13[e, m][:, :, :VEC_COLS])
+                interleave(nc.scalar.copy, grouped[:, VEC_COLS:, :], raw13[e, m][:, :, VEC_COLS:])
 
         def product13(e, m):
             slots = slice(e * C, (e + 1) * C)
             w_words = ring3.tile([P, H], U32, name="w_words", align_bytes=64)
             w_scales = ring3.tile([P, H], U8, name="w_scales", align_bytes=64)
-            nc.vector.quantize_mx(out=w_words[:].bitcast(FP8X4), scales=w_scales[:], in_=stage[m][:])
             sums[e, m] = acc.tile([P, H], F32, name="sums", tag="acc")
-            nc.tensor.matmul_mx(out=sums[e, m][:], lhsT=slot_words[:, slots].bitcast(FP8X4), lhsT_scale=slot_scales[:, slots],
-                                rhs=w_words[:].bitcast(FP8X4), rhs_scale=w_scales[:], start=True, stop=True)
+            parts = 2 if (e, m) == (E - 1, 1) else 1
+            for a in range(parts):
+                cols = slice(a * H // parts, (a + 1) * H // parts)
+                nc.vector.quantize_mx(out=w_words[:, cols].bitcast(FP8X4), scales=w_scales[:, cols], in_=stage[m][:, cols.start * PACK : cols.stop * PACK])
+                nc.tensor.matmul_mx(out=sums[e, m][:, cols], lhsT=slot_words[:, slots].bitcast(FP8X4), lhsT_scale=slot_scales[:, slots],
+                                    rhs=w_words[:, cols].bitcast(FP8X4), rhs_scale=w_scales[:, cols], start=True, stop=True)
+
+        def activate(e, place):
+            acts[e] = place
+            nc.scalar.activation(place, sums[e, 0][:], GELU)
 
         def hidden_rows(e, pairs):
-            nc.vector.tensor_tensor(pairs.bitcast(BF16), sums[e, 1][:], raw13[e, 1][:, PACK - 1, :], MULT)
+            nc.vector.tensor_tensor(pairs.bitcast(BF16), sums[e, 1][:], acts[e], MULT)
             turned[e] = turn.tile([P, 2, C], F32, name="turned")
             for u in range(2):
                 nc.tensor.transpose(turned[e][:, u, :], pairs[:, u : H // 2 : 2], ident[:])
@@ -125,46 +146,53 @@ def tile_moe_cpy_glu_gelu_kernel(tc, x_words, x_scales, xr, w1, w3, w2, gate, of
             nc.scalar.copy(pairs.rearrange("p (s u) -> p s u", u=2), turned[e][:].rearrange("p u s -> p s u"))
             nc.vector.quantize_mx(out=h_words[:, slots].bitcast(FP8X4), scales=h_scales[:, slots], in_=pairs.bitcast(BF16))
 
-        for e in range(E):
+        for e in range(E - 1):
             cast13(e, 0)
-            if e > 0:
-                hidden_rows(e - 1, raw13[e, 0][:, 0, : H // 2])
             product13(e, 0)
+            if e > 0:
+                activate(e - 1, raw13[e, 0][:, PACK - 1, :])
+                hidden_rows(e - 1, raw13[e, 0][:, 0, : H // 2])
             cast13(e, 1)
-            nc.scalar.activation(raw13[e, 1][:, PACK - 1, :], sums[e, 0][:], GELU)
             product13(e, 1)
             if e > 0:
                 hidden_codes(e - 1, raw13[e, 1][:, PACK - 2, H // 2 :])
+        activate(E - 2, raw13[E - 2, 1][:, PACK - 1, :])
+        cast13(E - 1, 0)
+        hidden_rows(E - 2, raw13[E - 1, 0][:, 0, : H // 2])
+        product13(E - 1, 0)
+        cast13(E - 1, 1)
+        hidden_codes(E - 2, last_halves[0][:, 1, :])
+        activate(E - 1, last_halves[0][:, 2:, :].rearrange("p j c -> p (j c)"))
+        product13(E - 1, 1)
 
         codes2 = {}
 
         def cast2(b, e):
-            flat, u = (stage[b % 2], e) if e < 4 else (stage_b[b % 2], e - 4)
-            grouped = flat[:].rearrange("p (c j) -> p c j", j=PACK)
-            copy = nc.vector.tensor_copy if (b == 0 and e in (0, 1, 5)) else nc.scalar.copy
-            interleave(copy, grouped[:, u * P : (u + 1) * P, :], raw2[b][:, e, :, :])
+            flat, u = (stage[b % 2][:], e) if e < 4 else (stage_b[b % 2], e - 4)
+            grouped = flat.rearrange("p (c j) -> p c j", j=PACK)
+            copy = nc.vector.tensor_copy if (b == 0 and e in (0, 5)) else nc.scalar.copy
+            interleave(copy, grouped[:, u * P : (u + 1) * P, :], raw2[b, e])
 
         def product2(b, experts):
             w2_words, w2_scales, banks = codes2[b]
             cols = slice(experts[0] * P, (experts[-1] + 1) * P)
-            flat = stage[b % 2] if experts[0] == 0 else stage_b[b % 2]
-            nc.vector.quantize_mx(out=w2_words[:, cols].bitcast(FP8X4), scales=w2_scales[:, cols], in_=flat[:])
+            flat = stage[b % 2][:] if experts[0] == 0 else stage_b[b % 2]
+            nc.vector.quantize_mx(out=w2_words[:, cols].bitcast(FP8X4), scales=w2_scales[:, cols], in_=flat)
             for e in experts:
                 slots = slice(e * C, (e + 1) * C)
-                nc.tensor.matmul_mx(out=banks[e % 2][:, e // 2, :], lhsT=w2_words[:, slots].bitcast(FP8X4), lhsT_scale=w2_scales[:, slots],
+                nc.tensor.matmul_mx(out=banks[e // 4][:, (e % 4) * C : (e % 4 + 1) * C], lhsT=w2_words[:, slots].bitcast(FP8X4), lhsT_scale=w2_scales[:, slots],
                                     rhs=h_words[:, slots].bitcast(FP8X4), rhs_scale=h_scales[:, slots], start=True, stop=True)
 
         def open_block(b):
             w2_words = ring2.tile([P, SLOTS], U32, name="w2_words", align_bytes=64)
             w2_scales = ring2.tile([P, SLOTS], U8, name="w2_scales", align_bytes=64)
-            banks = [acc.tile([P, E // 2, C], F32, name=f"y_sums{i}", tag="acc") for i in range(2)]
+            banks = [acc.tile([P, width], F32, name=f"y_sums{width}", tag="acc") for width in (4 * C, 2 * C)]
             codes2[b] = (w2_words, w2_scales, banks)
 
         def close_block(b):
-            by_pair = window[b][:, :SLOTS].rearrange("p (a u s) -> p a u s", u=2, s=C)
-            for u in range(2):
-                copy = nc.vector.tensor_copy if (b, u) == (0, 1) else nc.scalar.copy
-                copy(by_pair[:, :, u, :], codes2[b][2][u][:])
+            banks = codes2[b][2]
+            nc.scalar.copy(window[b][:, : 4 * C], banks[0][:])
+            (nc.vector.tensor_copy if b == 0 else nc.scalar.copy)(window[b][:, 4 * C : SLOTS], banks[1][:])
 
         def first_four(b):
             open_block(b)
@@ -179,12 +207,12 @@ def tile_moe_cpy_glu_gelu_kernel(tc, x_words, x_scales, xr, w1, w3, w2, gate, of
             close_block(b)
 
         def spent(e):
-            return raw2[0][:, e, 0:2, :].rearrange("p j n -> p (j n)")
+            return raw2[0, e][:, 0:2, :].rearrange("p j n -> p (j n)")
 
         open_block(0)
         cast2(0, 0)
+        hidden_rows(E - 1, spent(0))
         cast2(0, 1)
-        hidden_rows(E - 1, spent(1))
         cast2(0, 2)
         cast2(0, 3)
         product2(0, range(4))
@@ -193,27 +221,40 @@ def tile_moe_cpy_glu_gelu_kernel(tc, x_words, x_scales, xr, w1, w3, w2, gate, of
         cast2(0, 5)
         product2(0, range(4, E))
         close_block(0)
+        picked = {}
+        two = {}
+
+        def fetch(b, r, cols=slice(0, T)):
+            offsets = pos_sb[r][:, cols.start // 16 : cols.stop // 16]
+            nc.vector.tensor_tensor(picked[b, r][:, cols], window[b][:].indirect(offsets), gates[:, r, cols], MULT)
+
+        def finish(b, total, cols=slice(0, T)):
+            nc.vector.tensor_tensor(total[:, cols], two[b][:, cols], picked[b, 2][:, cols], ADD)
+            nc.sync.dma_start(out[b * P : (b + 1) * P, cols], total[:, cols])
+
         for b in range(BLOCKS):
-            more = b + 1 < BLOCKS
             spare = (b + 1) % 2
-            picked0 = ring2.tile([P, T], F32, name="picked0")
-            picked1 = ring2.tile([P, T], F32, name="picked1")
-            picked2 = stage[spare][:, : 2 * T].bitcast(F32)
-            two = stage_b[spare][:].bitcast(F32)
-            nc.vector.tensor_tensor(picked0[:], window[b][:].indirect(pos_sb[0][:]), gates[:, 0, :], MULT)
-            nc.vector.tensor_tensor(picked1[:], window[b][:].indirect(pos_sb[1][:]), gates[:, 1, :], MULT)
-            if more:
+            picked[b, 0] = ring2.tile([P, T], F32, name="picked0")[:]
+            picked[b, 1] = ring2.tile([P, T], F32, name="picked1")[:]
+            picked[b, 2] = wide[spare][:, : 2 * T].bitcast(F32)
+            two[b] = wide[spare][:, 2 * T :].bitcast(F32)
+            if b + 1 < BLOCKS:
+                fetch(b, 0)
+                fetch(b, 1)
                 first_four(b + 1)
-            nc.vector.tensor_tensor(picked2, window[b][:].indirect(pos_sb[2][:]), gates[:, 2, :], MULT)
-            if more:
+                if b > 0:
+                    finish(b - 1, stage[spare][:, : 2 * T].bitcast(F32))
                 last_two(b + 1)
-            total = ring2.tile([P, T], F32, name="total")
-            halves = (slice(0, T // 2), slice(T // 2, T))
-            for cols in halves:
-                nc.vector.tensor_tensor(two[:, cols], picked0[:, cols], picked1[:, cols], ADD)
-            for cols in halves:
-                nc.vector.tensor_tensor(total[:, cols], two[:, cols], picked2[:, cols], ADD)
-                if not more:
-                    nc.sync.dma_start(out[b * P : (b + 1) * P, cols], total[:, cols])
-            if more:
-                nc.sync.dma_start(out[b * P : (b + 1) * P, :], total[:])
+                fetch(b, 2)
+                nc.vector.tensor_tensor(two[b], picked[b, 0], picked[b, 1], ADD)
+            else:
+                left, right = slice(0, T // 2), slice(T // 2, T)
+                fetch(b, 0)
+                finish(b - 1, ring2.tile([P, T], F32, name="total")[:])
+                fetch(b, 1)
+                fetch(b, 2, left)
+                nc.vector.tensor_tensor(two[b], picked[b, 0], picked[b, 1], ADD)
+                fetch(b, 2, right)
+                total = ring2.tile([P, T], F32, name="total")[:]
+                finish(b, total, left)
+                finish(b, total, right)

@@ -45,9 +45,6 @@ def tile_moe_cpy_glu_gelu_kernel(tc, x_words, x_scales, xr, w1, w3, w2, gate, of
             nc.sync.dma_start(tok_scales[32 * q : 32 * q + 4, :].bitcast(I32), x_scales[0, 4 * q : 4 * q + 4, :].bitcast(I32))
         gate_cols = keep.tile([P, TOP, 4], F32, name="gate_cols")
         nc.scalar.dma_start(gate_cols[:], gate[:, 0, :].rearrange("r (p c) -> p r c", c=4))
-        warm = keep.tile([P, 16], F32, name="warm")
-        nc.vector.memset(warm[:, :8], 0.0)
-        nc.scalar.activation(warm[:, 8:], warm[:, :8], GELU)
 
         raw13 = {}
         last_halves = []

@@ -22,8 +22,8 @@ GELU = mybir.ActivationFunctionType.Gelu_apprx_tanh
 P = 128
 PACK = 4
 BLOCKS = K // P
-PAIR = 2 * C
-VEC_COLS = 256
+WHOLE = 2
+VEC_COLS = 320
 
 
 def tile_moe_cpy_glu_gelu_kernel(tc, x_words, x_scales, xr, w1, w3, w2, gate, offs, pos1, pos2, pos3, out):
@@ -32,8 +32,8 @@ def tile_moe_cpy_glu_gelu_kernel(tc, x_words, x_scales, xr, w1, w3, w2, gate, of
         keep = ctx.enter_context(tc.tile_pool(name="keep", bufs=1))
         ring3 = ctx.enter_context(tc.tile_pool(name="ring3", bufs=3))
         ring2 = ctx.enter_context(tc.tile_pool(name="ring2", bufs=2))
-        acc = ctx.enter_context(tc.psum_pool(name="acc", bufs=6))
-        turn = ctx.enter_context(tc.psum_pool(name="turn", bufs=2))
+        acc = ctx.enter_context(tc.psum_pool(name="acc", bufs=4))
+        held = ctx.enter_context(tc.psum_pool(name="held", bufs=1))
 
         offs_sb = keep.tile([P, SLOTS // 16], U16, name="offs_sb")
         nc.sync.dma_start(offs_sb[:], offs)
@@ -47,33 +47,37 @@ def tile_moe_cpy_glu_gelu_kernel(tc, x_words, x_scales, xr, w1, w3, w2, gate, of
         nc.scalar.dma_start(gate_cols[:], gate[:, 0, :].rearrange("r (p c) -> p r c", c=4))
 
         raw13 = {}
-        last_halves = []
         pos_sb = []
         for e in range(E):
             for m, w in enumerate((w1, w3)):
-                rows = w[e].rearrange("(p j) c -> p j c", j=PACK)
-                if (e, m) == (E - 1, 1):
-                    for a in range(2):
-                        last_halves.append(keep.tile([P, PACK, H // 2], F32, name=f"last_half{a}", align_bytes=64))
-                        nc.sync.dma_start(last_halves[a][:], rows[:, :, a * H // 2 : (a + 1) * H // 2])
-                else:
-                    raw13[e, m] = keep.tile([P, PACK, H], F32, name=f"raw13_{e}_{m}", align_bytes=64)
-                    nc.sync.dma_start(raw13[e, m][:], rows)
-            if e == 0:
-                for r, pos in enumerate((pos1, pos2, pos3)):
-                    pos_sb.append(keep.tile([P, T // 16], U16, name=f"pos_sb{r}"))
-                    nc.sync.dma_start(pos_sb[r][:], pos)
+                raw13[e, m] = keep.tile([P, PACK, H], F32, name=f"raw13_{e}_{m}", align_bytes=64)
+                nc.sync.dma_start(raw13[e, m][:], w[e].rearrange("(p j) c -> p j c", j=PACK))
+        whole2 = []
+        for e in range(WHOLE):
+            whole2.append(keep.tile([P, PACK, K], F32, name=f"whole2_{e}", align_bytes=64))
+            nc.sync.dma_start(whole2[e][:], w2[e].rearrange("(p j) n -> p j n", j=PACK))
         raw2 = {}
         window = []
         for b in range(BLOCKS):
             window.append(keep.tile([P, WIN], F32, name=f"window{b}", align_bytes=64))
-            landing = keep.tile([P, E, PACK, P], F32, name=f"landing{b}", align_bytes=64)
-            for e in range(E):
-                lodger = e == (4 if b == 0 else 5)
-                raw2[b, e] = window[b][:, : 4 * C].rearrange("p (j n) -> p j n", j=PACK) if lodger else landing[:, e, :, :]
-                nc.sync.dma_start(raw2[b, e], w2[e].rearrange("(p j) n -> p j n", j=PACK)[:, :, b * P : (b + 1) * P])
-            nc.sync.dma_start(window[b][:, SLOTS : SLOTS + T], xr[b * P : (b + 1) * P, :])
             nc.gpsimd.memset(window[b][:, SLOTS + T :], 0.0)
+        hosts = {(0, 3): 0, (1, 2): 1, (1, 3): 2, (2, 2): 3}
+        for b in range(BLOCKS):
+            pair = keep.tile([P, 2, PACK, P], F32, name=f"pair{b}", align_bytes=64)
+            raw2[b, "pair"] = pair[:]
+            for u in range(E - WHOLE):
+                if u < 2:
+                    raw2[b, u] = pair[:, u, :, :]
+                elif (b, u) in hosts:
+                    raw2[b, u] = window[hosts[b, u]][:, : PACK * P].rearrange("p (j n) -> p j n", j=PACK)
+                else:
+                    raw2[b, u] = keep.tile([P, PACK, P], F32, name=f"raw2_{b}_{u}", align_bytes=64)[:]
+                nc.sync.dma_start(raw2[b, u], w2[WHOLE + u].rearrange("(p j) n -> p j n", j=PACK)[:, :, b * P : (b + 1) * P])
+            nc.sync.dma_start(window[b][:, SLOTS : SLOTS + T], xr[b * P : (b + 1) * P, :])
+            if b == 0:
+                for r, pos in enumerate((pos1, pos2, pos3)):
+                    pos_sb.append(keep.tile([P, T // 16], U16, name=f"pos_sb{r}"))
+                    nc.sync.dma_start(pos_sb[r][:], pos)
 
         ident = keep.tile([P, P], F32, name="ident")
         make_identity(nc, ident[:])
@@ -88,7 +92,7 @@ def tile_moe_cpy_glu_gelu_kernel(tc, x_words, x_scales, xr, w1, w3, w2, gate, of
 
         gates = keep.tile([P, TOP, T], F32, name="gates")
         for r in range(TOP):
-            spread = acc.tile([P, 4, P], F32, name="spread", tag="acc")
+            spread = held.tile([P, 4, P], F32, name="spread", tag=f"held{r}")
             for c in range(4):
                 nc.tensor.transpose(spread[:, c, :], gate_cols[:, r, c : c + 1].to_broadcast([P, P]), ident[:])
             nc.scalar.copy(gates[:, r, :].rearrange("p (n c) -> p n c", c=4), spread[:].rearrange("p c n -> p n c"))
@@ -100,158 +104,174 @@ def tile_moe_cpy_glu_gelu_kernel(tc, x_words, x_scales, xr, w1, w3, w2, gate, of
         h_scales = keep.tile([P, SLOTS], U8, name="h_scales", align_bytes=64)
 
         stage = [keep.tile([P, H * PACK], BF16, name=f"stage{i}", align_bytes=64) for i in range(2)]
-        wide = [keep.tile([P, 4 * T], BF16, name=f"wide{i}", align_bytes=64) for i in range(2)]
-        stage_b = [wide[i][:, T : 3 * T] for i in range(2)]
         sums = {}
-        turned = {}
-
         acts = {}
+        rounded = {}
 
         def cast13(e, m):
-            grouped = stage[m][:].rearrange("p (c j) -> p c j", j=PACK)
-            if (e, m) == (E - 1, 1):
-                interleave(nc.scalar.copy, grouped[:, : H // 2, :], last_halves[0][:])
-                interleave(nc.vector.tensor_copy, grouped[:, H // 2 :, :], last_halves[1][:])
-            else:
-                interleave(nc.vector.tensor_copy, grouped[:, :VEC_COLS, :], raw13[e, m][:, :, :VEC_COLS])
-                interleave(nc.scalar.copy, grouped[:, VEC_COLS:, :], raw13[e, m][:, :, VEC_COLS:])
+            copy = (nc.vector.tensor_copy, nc.scalar.copy)[m]
+            copy(stage[m][:].rearrange("p (t c j) -> p c j t", t=PACK, j=PACK), raw13[e, m][:].rearrange("p j (c t) -> p c j t", t=PACK))
+
+        def codes(m):
+            w_words = ring3.tile([P, H], U32, name="w_words", align_bytes=64)
+            w_scales = ring3.tile([P, H], U8, name="w_scales", align_bytes=64)
+            nc.vector.quantize_mx(out=w_words[:].bitcast(FP8X4), scales=w_scales[:], in_=stage[m][:])
+            return w_words, w_scales
 
         def product13(e, m):
             slots = slice(e * C, (e + 1) * C)
-            w_words = ring3.tile([P, H], U32, name="w_words", align_bytes=64)
-            w_scales = ring3.tile([P, H], U8, name="w_scales", align_bytes=64)
-            sums[e, m] = acc.tile([P, H], F32, name="sums", tag="acc")
-            parts = 2 if (e, m) == (E - 1, 1) else 1
-            for a in range(parts):
-                cols = slice(a * H // parts, (a + 1) * H // parts)
-                nc.vector.quantize_mx(out=w_words[:, cols].bitcast(FP8X4), scales=w_scales[:, cols], in_=stage[m][:, cols.start * PACK : cols.stop * PACK])
-                nc.tensor.matmul_mx(out=sums[e, m][:, cols], lhsT=slot_words[:, slots].bitcast(FP8X4), lhsT_scale=slot_scales[:, slots],
-                                    rhs=w_words[:, cols].bitcast(FP8X4), rhs_scale=w_scales[:, cols], start=True, stop=True)
+            w_words, w_scales = codes(m)
+            sums[e, m] = acc.tile([P, PACK, C], F32, name="sums", tag="acc")
+            for t in range(PACK):
+                cols = slice(t * P, (t + 1) * P)
+                nc.tensor.matmul_mx(out=sums[e, m][:, t, :], lhsT=w_words[:, cols].bitcast(FP8X4), lhsT_scale=w_scales[:, cols],
+                                    rhs=slot_words[:, slots].bitcast(FP8X4), rhs_scale=slot_scales[:, slots], start=True, stop=True)
 
         def activate(e, place):
-            acts[e] = place
-            nc.scalar.activation(place, sums[e, 0][:], GELU)
+            acts[e] = place.rearrange("p (s t) -> p s t", t=PACK)
+            nc.scalar.activation(acts[e], sums[e, 0][:].rearrange("p t s -> p s t"), GELU)
 
-        def hidden_rows(e, pairs):
-            nc.vector.tensor_tensor(pairs.bitcast(BF16), sums[e, 1][:], acts[e], MULT)
-            turned[e] = turn.tile([P, 2, C], F32, name="turned")
-            for u in range(2):
-                nc.tensor.transpose(turned[e][:, u, :], pairs[:, u : H // 2 : 2], ident[:])
+        def hidden(e, place):
+            rounded[e] = place.bitcast(BF16)
+            nc.vector.tensor_tensor(rounded[e].rearrange("p (s t) -> p s t", t=PACK), sums[e, 1][:].rearrange("p t s -> p s t"), acts[e], MULT)
 
-        def hidden_codes(e, pairs):
+        def hidden_codes(e):
             slots = slice(e * C, (e + 1) * C)
-            nc.scalar.copy(pairs.rearrange("p (s u) -> p s u", u=2), turned[e][:].rearrange("p u s -> p s u"))
-            nc.vector.quantize_mx(out=h_words[:, slots].bitcast(FP8X4), scales=h_scales[:, slots], in_=pairs.bitcast(BF16))
+            nc.vector.quantize_mx(out=h_words[:, slots].bitcast(FP8X4), scales=h_scales[:, slots], in_=rounded[e])
 
-        for e in range(E - 1):
+        for e in range(E):
             cast13(e, 0)
+            if e > 0:
+                hidden(e - 1, raw13[e, 0][:, 0, : H // 2])
             product13(e, 0)
             if e > 0:
-                activate(e - 1, raw13[e, 0][:, PACK - 1, :])
-                hidden_rows(e - 1, raw13[e, 0][:, 0, : H // 2])
+                hidden_codes(e - 1)
             cast13(e, 1)
+            activate(e, raw13[e, 1][:, PACK - 1, :])
             product13(e, 1)
-            if e > 0:
-                hidden_codes(e - 1, raw13[e, 1][:, PACK - 2, H // 2 :])
-        activate(E - 2, raw13[E - 2, 1][:, PACK - 1, :])
-        cast13(E - 1, 0)
-        hidden_rows(E - 2, raw13[E - 1, 0][:, 0, : H // 2])
-        product13(E - 1, 0)
-        cast13(E - 1, 1)
-        hidden_codes(E - 2, last_halves[0][:, 1, :])
-        activate(E - 1, last_halves[0][:, 2:, :].rearrange("p j c -> p (j c)"))
-        product13(E - 1, 1)
 
-        codes2 = {}
+        def second(out_cols, words, scales, cols, e):
+            slots = slice(e * C, (e + 1) * C)
+            nc.tensor.matmul_mx(out=out_cols, lhsT=words[:, cols].bitcast(FP8X4), lhsT_scale=scales[:, cols],
+                                rhs=h_words[:, slots].bitcast(FP8X4), rhs_scale=h_scales[:, slots], start=True, stop=True)
 
-        def cast2(b, e):
-            flat, u = (stage[b % 2][:], e) if e < 4 else (stage_b[b % 2], e - 4)
-            grouped = flat.rearrange("p (c j) -> p c j", j=PACK)
-            copy = nc.vector.tensor_copy if (b == 0 and e in (0, 5)) else nc.scalar.copy
-            interleave(copy, grouped[:, u * P : (u + 1) * P, :], raw2[b, e])
+        early = [acc.tile([P, 2, WHOLE * C], F32, name="early", tag="acc") for i in range(2)]
+        for e in range(WHOLE):
+            grouped = stage[e][:].rearrange("p (c j) -> p c j", j=PACK)
+            interleave(nc.vector.tensor_copy, grouped[:, :VEC_COLS, :], whole2[e][:, :, :VEC_COLS])
+            interleave(nc.scalar.copy, grouped[:, VEC_COLS:, :], whole2[e][:, :, VEC_COLS:])
+            if e == 0:
+                hidden(E - 1, whole2[e][:, 0, : H // 2])
+            w_words, w_scales = codes(e)
+            if e == 0:
+                hidden_codes(E - 1)
+            for b in range(BLOCKS):
+                second(early[b // 2][:, b % 2, e * C : (e + 1) * C], w_words, w_scales, slice(b * P, (b + 1) * P), e)
 
-        def product2(b, experts):
-            w2_words, w2_scales, banks = codes2[b]
-            cols = slice(experts[0] * P, (experts[-1] + 1) * P)
-            flat = stage[b % 2][:] if experts[0] == 0 else stage_b[b % 2]
-            nc.vector.quantize_mx(out=w2_words[:, cols].bitcast(FP8X4), scales=w2_scales[:, cols], in_=flat)
-            for e in experts:
-                slots = slice(e * C, (e + 1) * C)
-                nc.tensor.matmul_mx(out=banks[e // 4][:, (e % 4) * C : (e % 4 + 1) * C], lhsT=w2_words[:, slots].bitcast(FP8X4), lhsT_scale=w2_scales[:, slots],
-                                    rhs=h_words[:, slots].bitcast(FP8X4), rhs_scale=h_scales[:, slots], start=True, stop=True)
+        def empty_early(b):
+            nc.scalar.copy(window[b][:, : WHOLE * C], early[b // 2][:, b % 2, :])
 
-        def open_block(b):
-            w2_words = ring2.tile([P, SLOTS], U32, name="w2_words", align_bytes=64)
-            w2_scales = ring2.tile([P, SLOTS], U8, name="w2_scales", align_bytes=64)
-            banks = [acc.tile([P, width], F32, name=f"y_sums{width}", tag="acc") for width in (4 * C, 2 * C)]
-            codes2[b] = (w2_words, w2_scales, banks)
+        last = BLOCKS - 1
+        HALF = 2 * P * PACK
+        wide = {b: keep.tile([P, HALF + 3 * HALF // 4], BF16, name=f"wide{b}", align_bytes=64) for b in range(1, BLOCKS)}
+        alone = {key: keep.tile([P, HALF], BF16, name=f"alone{key[0]}{key[1]}", align_bytes=64)[:] for key in ((0, 0), (0, 1), (1, 0))}
 
-        def close_block(b):
-            banks = codes2[b][2]
-            nc.scalar.copy(window[b][:, : 4 * C], banks[0][:])
-            (nc.vector.tensor_copy if b == 0 else nc.scalar.copy)(window[b][:, 4 * C : SLOTS], banks[1][:])
+        def staged(b, a):
+            if (b, a) in alone:
+                return alone[b, a]
+            return wide[b][:, :HALF] if a == 1 else wide[b - 1][:, 3 * HALF // 4 :]
 
-        def first_four(b):
-            open_block(b)
-            for e in range(4):
-                cast2(b, e)
-            product2(b, range(4))
+        def cast2(b):
+            nc.scalar.copy(staged(b, 0).rearrange("p (u c i j) -> p u c j i", u=2, i=4, j=PACK), raw2[b, "pair"].rearrange("p u j (c i) -> p u c j i", i=4))
+            for u in range(2):
+                interleave(nc.scalar.copy, staged(b, 1).rearrange("p (c j) -> p c j", j=PACK)[:, u * P : (u + 1) * P, :], raw2[b, 2 + u])
 
-        def last_two(b):
-            for e in range(4, E):
-                cast2(b, e)
-            product2(b, range(4, E))
-            close_block(b)
+        def product2(b):
+            w2_words = ring2.tile([P, 4 * P], U32, name="w2_words", align_bytes=64)
+            w2_scales = ring2.tile([P, 4 * P], U8, name="w2_scales", align_bytes=64)
+            if b < last:
+                bank = acc.tile([P, 4 * C], F32, name="y_sums", tag="acc")
+            else:
+                bank = held.tile([P, 4 * C], F32, name="y_last", tag="held3")
+            for a in range(2):
+                cols = slice(2 * a * P, 2 * (a + 1) * P)
+                nc.vector.quantize_mx(out=w2_words[:, cols].bitcast(FP8X4), scales=w2_scales[:, cols], in_=staged(b, a))
+                for u in range(2 * a, 2 * a + 2):
+                    second(bank[:, u * C : (u + 1) * C], w2_words, w2_scales, slice(u * P, (u + 1) * P), WHOLE + u)
+            (nc.vector.tensor_copy if b == 0 else nc.scalar.copy)(window[b][:, WHOLE * C : SLOTS], bank[:])
 
-        def spent(e):
-            return raw2[0, e][:, 0:2, :].rearrange("p j n -> p (j n)")
-
-        open_block(0)
-        cast2(0, 0)
-        hidden_rows(E - 1, spent(0))
-        cast2(0, 1)
-        cast2(0, 2)
-        cast2(0, 3)
-        product2(0, range(4))
-        cast2(0, 4)
-        hidden_codes(E - 1, spent(4))
-        cast2(0, 5)
-        product2(0, range(4, E))
-        close_block(0)
         picked = {}
-        two = {}
+        summed = {}
+        summed_sb = {}
 
         def fetch(b, r, cols=slice(0, T)):
             offsets = pos_sb[r][:, cols.start // 16 : cols.stop // 16]
             nc.vector.tensor_tensor(picked[b, r][:, cols], window[b][:].indirect(offsets), gates[:, r, cols], MULT)
 
-        def finish(b, total, cols=slice(0, T)):
-            nc.vector.tensor_tensor(total[:, cols], two[b][:, cols], picked[b, 2][:, cols], ADD)
-            nc.sync.dma_start(out[b * P : (b + 1) * P, cols], total[:, cols])
+        def add_turned(b):
+            if b < 2:
+                bank = held.tile([P, T // P, P], F32, name="summed", tag=f"held{b}")
+                summed[b] = [bank[:, c, :] for c in range(T // P)]
+                summed[b, "bank"] = bank[:].rearrange("p c n -> p (c n)")
+            else:
+                summed[b] = [acc.tile([P, P], F32, name="summed_part", tag="acc")[:] for c in range(T // P)]
+            for c in reversed(range(T // P)):
+                for r in range(TOP):
+                    nc.tensor.matmul(summed[b][c], lhsT=picked[b, r][:, c * P : (c + 1) * P], rhs=ident[:], is_transpose=True, start=r == 0, stop=r == TOP - 1)
 
+        def empty_turned(b, place):
+            summed_sb[b] = place
+            if b < 2:
+                nc.scalar.copy(place, summed[b, "bank"])
+            else:
+                for c in reversed(range(T // P)):
+                    nc.scalar.copy(place[:, c * P : (c + 1) * P], summed[b][c])
+
+        def turn_back(b, tag):
+            back = held.tile([P, T], F32, name="back", tag=tag)
+            for c in range(T // P):
+                nc.tensor.transpose(back[:, c * P : (c + 1) * P], summed_sb[b][:, c * P : (c + 1) * P], ident[:])
+            total = raw13[b, 0][:, 1, :]
+            nc.scalar.copy(total, back[:])
+            nc.scalar.dma_start(out[b * P : (b + 1) * P, :], total)
+
+        left, right = slice(0, T // 2), slice(T // 2, T)
+        cast2(0)
+        empty_early(0)
+        product2(0)
         for b in range(BLOCKS):
-            spare = (b + 1) % 2
             picked[b, 0] = ring2.tile([P, T], F32, name="picked0")[:]
             picked[b, 1] = ring2.tile([P, T], F32, name="picked1")[:]
-            picked[b, 2] = wide[spare][:, : 2 * T].bitcast(F32)
-            two[b] = wide[spare][:, 2 * T :].bitcast(F32)
-            if b + 1 < BLOCKS:
-                fetch(b, 0)
-                fetch(b, 1)
-                first_four(b + 1)
-                if b > 0:
-                    finish(b - 1, stage[spare][:, : 2 * T].bitcast(F32))
-                last_two(b + 1)
-                fetch(b, 2)
-                nc.vector.tensor_tensor(two[b], picked[b, 0], picked[b, 1], ADD)
+            fetch(b, 0)
+            fetch(b, 1)
+            if b == last:
+                break
+            cast2(b + 1)
+            if b == 0:
+                empty_early(1)
+                empty_early(2)
             else:
-                left, right = slice(0, T // 2), slice(T // 2, T)
-                fetch(b, 0)
-                finish(b - 1, ring2.tile([P, T], F32, name="total")[:])
-                fetch(b, 1)
-                fetch(b, 2, left)
-                nc.vector.tensor_tensor(two[b], picked[b, 0], picked[b, 1], ADD)
+                if b == 1:
+                    empty_early(3)
+                empty_turned(b - 1, raw2[b + 1, 3].rearrange("p j n -> p (j n)"))
+            product2(b + 1)
+            picked[b, 2] = staged(b + 1, 1).bitcast(F32)
+            if b < 2:
                 fetch(b, 2, right)
-                total = ring2.tile([P, T], F32, name="total")[:]
-                finish(b, total, left)
-                finish(b, total, right)
+                fetch(b, 2, left)
+            else:
+                fetch(b, 2)
+            add_turned(b)
+        turn_back(0, "held3")
+        empty_turned(2, raw13[2, 0][:, 2, :])
+        turn_back(1, "held3")
+        turn_back(2, "held0")
+        picked[last, 2] = raw13[last, 0][:, 3, :]
+        two = raw13[last, 0][:, 2, :]
+        total = raw13[last, 0][:, 1, :]
+        fetch(last, 2, left)
+        nc.vector.tensor_tensor(two, picked[last, 0], picked[last, 1], ADD)
+        fetch(last, 2, right)
+        for cols in (left, right):
+            nc.vector.tensor_tensor(total[:, cols], two[:, cols], picked[last, 2][:, cols], ADD)
+            nc.sync.dma_start(out[last * P :, cols], total[:, cols])

@@ -23,7 +23,7 @@ P = 128
 PACK = 4
 BLOCKS = K // P
 WHOLE = 2
-VEC_COLS = 320
+VEC_COLS = 128
 
 
 def tile_moe_cpy_glu_gelu_kernel(tc, x_words, x_scales, xr, w1, w3, w2, gate, offs, pos1, pos2, pos3, out):
@@ -105,12 +105,16 @@ def tile_moe_cpy_glu_gelu_kernel(tc, x_words, x_scales, xr, w1, w3, w2, gate, of
 
         stage = [keep.tile([P, H * PACK], BF16, name=f"stage{i}", align_bytes=64) for i in range(2)]
         sums = {}
+        turned = {}
         acts = {}
-        rounded = {}
 
         def cast13(e, m):
-            copy = (nc.vector.tensor_copy, nc.scalar.copy)[m]
-            copy(stage[m][:].rearrange("p (t c j) -> p c j t", t=PACK, j=PACK), raw13[e, m][:].rearrange("p j (c t) -> p c j t", t=PACK))
+            grouped = stage[m][:].rearrange("p (c j) -> p c j", j=PACK)
+            if (e, m) == (E - 1, 1):
+                interleave(nc.scalar.copy, grouped[:, VEC_COLS:, :], raw13[e, m][:, :, VEC_COLS:])
+                interleave(nc.vector.tensor_copy, grouped[:, :VEC_COLS, :], raw13[e, m][:, :, :VEC_COLS])
+            else:
+                interleave((nc.vector.tensor_copy, nc.scalar.copy)[m], grouped, raw13[e, m][:])
 
         def codes(m):
             w_words = ring3.tile([P, H], U32, name="w_words", align_bytes=64)
@@ -121,34 +125,35 @@ def tile_moe_cpy_glu_gelu_kernel(tc, x_words, x_scales, xr, w1, w3, w2, gate, of
         def product13(e, m):
             slots = slice(e * C, (e + 1) * C)
             w_words, w_scales = codes(m)
-            sums[e, m] = acc.tile([P, PACK, C], F32, name="sums", tag="acc")
-            for t in range(PACK):
-                cols = slice(t * P, (t + 1) * P)
-                nc.tensor.matmul_mx(out=sums[e, m][:, t, :], lhsT=w_words[:, cols].bitcast(FP8X4), lhsT_scale=w_scales[:, cols],
-                                    rhs=slot_words[:, slots].bitcast(FP8X4), rhs_scale=slot_scales[:, slots], start=True, stop=True)
+            sums[e, m] = acc.tile([P, H], F32, name="sums", tag="acc")
+            nc.tensor.matmul_mx(out=sums[e, m][:], lhsT=slot_words[:, slots].bitcast(FP8X4), lhsT_scale=slot_scales[:, slots],
+                                rhs=w_words[:].bitcast(FP8X4), rhs_scale=w_scales[:], start=True, stop=True)
 
         def activate(e, place):
-            acts[e] = place.rearrange("p (s t) -> p s t", t=PACK)
-            nc.scalar.activation(acts[e], sums[e, 0][:].rearrange("p t s -> p s t"), GELU)
+            acts[e] = place
+            nc.scalar.activation(place, sums[e, 0][:], GELU)
 
-        def hidden(e, place):
-            rounded[e] = place.bitcast(BF16)
-            nc.vector.tensor_tensor(rounded[e].rearrange("p (s t) -> p s t", t=PACK), sums[e, 1][:].rearrange("p t s -> p s t"), acts[e], MULT)
+        def hidden_rows(e, pairs):
+            nc.vector.tensor_tensor(pairs.bitcast(BF16), sums[e, 1][:], acts[e], MULT)
+            turned[e] = held.tile([P, 2, C], F32, name="turned", tag=f"held{2 + e % 2}")
+            for u in range(2):
+                nc.tensor.transpose(turned[e][:, u, :], pairs[:, u : H // 2 : 2], ident[:])
 
-        def hidden_codes(e):
+        def hidden_codes(e, pairs):
             slots = slice(e * C, (e + 1) * C)
-            nc.vector.quantize_mx(out=h_words[:, slots].bitcast(FP8X4), scales=h_scales[:, slots], in_=rounded[e])
+            nc.scalar.copy(pairs.rearrange("p (s u) -> p s u", u=2), turned[e][:].rearrange("p u s -> p s u"))
+            nc.vector.quantize_mx(out=h_words[:, slots].bitcast(FP8X4), scales=h_scales[:, slots], in_=pairs.bitcast(BF16))
 
         for e in range(E):
             cast13(e, 0)
             if e > 0:
-                hidden(e - 1, raw13[e, 0][:, 0, : H // 2])
+                hidden_rows(e - 1, raw13[e, 0][:, 0, : H // 2])
             product13(e, 0)
-            if e > 0:
-                hidden_codes(e - 1)
             cast13(e, 1)
-            activate(e, raw13[e, 1][:, PACK - 1, :])
             product13(e, 1)
+            if e > 0:
+                hidden_codes(e - 1, raw13[e, 1][:, 0, H // 2 :])
+            activate(e, raw13[e, 1][:, PACK - 1, :])
 
         def second(out_cols, words, scales, cols, e):
             slots = slice(e * C, (e + 1) * C)
@@ -158,13 +163,14 @@ def tile_moe_cpy_glu_gelu_kernel(tc, x_words, x_scales, xr, w1, w3, w2, gate, of
         early = [acc.tile([P, 2, WHOLE * C], F32, name="early", tag="acc") for i in range(2)]
         for e in range(WHOLE):
             grouped = stage[e][:].rearrange("p (c j) -> p c j", j=PACK)
-            interleave(nc.vector.tensor_copy, grouped[:, :VEC_COLS, :], whole2[e][:, :, :VEC_COLS])
-            interleave(nc.scalar.copy, grouped[:, VEC_COLS:, :], whole2[e][:, :, VEC_COLS:])
             if e == 0:
-                hidden(E - 1, whole2[e][:, 0, : H // 2])
+                interleave(nc.vector.tensor_copy, grouped, whole2[e][:])
+                hidden_rows(E - 1, whole2[e][:, 0, : H // 2])
+            else:
+                interleave(nc.vector.tensor_copy, grouped[:, : K // 2, :], whole2[e][:, :, : K // 2])
+                interleave(nc.scalar.copy, grouped[:, K // 2 :, :], whole2[e][:, :, K // 2 :])
+                hidden_codes(E - 1, whole2[e][:, 0, K // 2 :])
             w_words, w_scales = codes(e)
-            if e == 0:
-                hidden_codes(E - 1)
             for b in range(BLOCKS):
                 second(early[b // 2][:, b % 2, e * C : (e + 1) * C], w_words, w_scales, slice(b * P, (b + 1) * P), e)
 
@@ -184,7 +190,7 @@ def tile_moe_cpy_glu_gelu_kernel(tc, x_words, x_scales, xr, w1, w3, w2, gate, of
         def cast2(b):
             nc.scalar.copy(staged(b, 0).rearrange("p (u c i j) -> p u c j i", u=2, i=4, j=PACK), raw2[b, "pair"].rearrange("p u j (c i) -> p u c j i", i=4))
             for u in range(2):
-                interleave(nc.scalar.copy, staged(b, 1).rearrange("p (c j) -> p c j", j=PACK)[:, u * P : (u + 1) * P, :], raw2[b, 2 + u])
+                interleave(nc.vector.tensor_copy if (b, u) == (0, 1) else nc.scalar.copy, staged(b, 1).rearrange("p (c j) -> p c j", j=PACK)[:, u * P : (u + 1) * P, :], raw2[b, 2 + u])
 
         def product2(b):
             w2_words = ring2.tile([P, 4 * P], U32, name="w2_words", align_bytes=64)

@@ -23,7 +23,9 @@ P = 128
 PACK = 4
 BLOCKS = K // P
 WHOLE = 2
-VEC_COLS = 128
+CUT = E - WHOLE
+VEC_COLS = (336, 336)
+VEC_13 = {(E - 2, 1): 144, (E - 1, 0): 336, (E - 1, 1): 256}
 
 
 def tile_moe_cpy_glu_gelu_kernel(tc, x_words, x_scales, xr, w1, w3, w2, gate, offs, pos1, pos2, pos3, out):
@@ -32,26 +34,38 @@ def tile_moe_cpy_glu_gelu_kernel(tc, x_words, x_scales, xr, w1, w3, w2, gate, of
         keep = ctx.enter_context(tc.tile_pool(name="keep", bufs=1))
         ring3 = ctx.enter_context(tc.tile_pool(name="ring3", bufs=3))
         ring2 = ctx.enter_context(tc.tile_pool(name="ring2", bufs=2))
-        acc = ctx.enter_context(tc.psum_pool(name="acc", bufs=4))
-        held = ctx.enter_context(tc.psum_pool(name="held", bufs=1))
+        psum = ctx.enter_context(tc.psum_pool(name="psum", bufs=1))
 
+        def bank(i, cols):
+            return psum.tile([P, cols], F32, name="bank", tag=f"bank{i}")
+
+        raw13 = {}
+
+        def load13(e, m):
+            raw13[e, m] = keep.tile([P, PACK, H], F32, name=f"raw13_{e}_{m}", align_bytes=64)
+            nc.sync.dma_start(raw13[e, m][:], (w1, w3)[m][e].rearrange("(p j) c -> p j c", j=PACK))
+
+        tok_scales = keep.tile([P, T], U8, name="tok_scales", align_bytes=64)
+        nc.gpsimd.memset(tok_scales[:].bitcast(I32), 0)
         offs_sb = keep.tile([P, SLOTS // 16], U16, name="offs_sb")
         nc.sync.dma_start(offs_sb[:], offs)
         tok_words = keep.tile([P, T], U32, name="tok_words", align_bytes=64)
         nc.sync.dma_start(tok_words[:].bitcast(I32), x_words[0].rearrange("p t d -> p (t d)").bitcast(I32))
-        tok_scales = keep.tile([P, T], U8, name="tok_scales", align_bytes=64)
-        nc.gpsimd.memset(tok_scales[:].bitcast(I32), 0)
+        load13(0, 0)
+        gate_cols = keep.tile([P, TOP, 4], F32, name="gate_cols")
+        nc.sync.dma_start(gate_cols[:], gate[:, 0, :].rearrange("r (p c) -> p r c", c=4))
         for q in range(4):
             nc.sync.dma_start(tok_scales[32 * q : 32 * q + 4, :].bitcast(I32), x_scales[0, 4 * q : 4 * q + 4, :].bitcast(I32))
-        gate_cols = keep.tile([P, TOP, 4], F32, name="gate_cols")
-        nc.scalar.dma_start(gate_cols[:], gate[:, 0, :].rearrange("r (p c) -> p r c", c=4))
-
-        raw13 = {}
+        load13(0, 1)
+        load13(1, 0)
+        load13(1, 1)
         pos_sb = []
-        for e in range(E):
-            for m, w in enumerate((w1, w3)):
-                raw13[e, m] = keep.tile([P, PACK, H], F32, name=f"raw13_{e}_{m}", align_bytes=64)
-                nc.sync.dma_start(raw13[e, m][:], w[e].rearrange("(p j) c -> p j c", j=PACK))
+        for e in range(2, E):
+            load13(e, 0)
+            load13(e, 1)
+            if e - 2 < TOP:
+                pos_sb.append(keep.tile([P, T // 16], U16, name=f"pos_sb{e - 2}"))
+                nc.sync.dma_start(pos_sb[e - 2][:], (pos1, pos2, pos3)[e - 2])
         whole2 = []
         for e in range(WHOLE):
             whole2.append(keep.tile([P, PACK, K], F32, name=f"whole2_{e}", align_bytes=64))
@@ -61,23 +75,14 @@ def tile_moe_cpy_glu_gelu_kernel(tc, x_words, x_scales, xr, w1, w3, w2, gate, of
         for b in range(BLOCKS):
             window.append(keep.tile([P, WIN], F32, name=f"window{b}", align_bytes=64))
             nc.gpsimd.memset(window[b][:, SLOTS + T :], 0.0)
-        hosts = {(0, 3): 0, (1, 2): 1, (1, 3): 2, (2, 2): 3}
         for b in range(BLOCKS):
-            pair = keep.tile([P, 2, PACK, P], F32, name=f"pair{b}", align_bytes=64)
-            raw2[b, "pair"] = pair[:]
-            for u in range(E - WHOLE):
-                if u < 2:
-                    raw2[b, u] = pair[:, u, :, :]
-                elif (b, u) in hosts:
-                    raw2[b, u] = window[hosts[b, u]][:, : PACK * P].rearrange("p (j n) -> p j n", j=PACK)
+            for u in range(CUT):
+                if b > 0 and u == CUT - 1:
+                    raw2[b, u] = window[b][:, : PACK * P]
                 else:
-                    raw2[b, u] = keep.tile([P, PACK, P], F32, name=f"raw2_{b}_{u}", align_bytes=64)[:]
-                nc.sync.dma_start(raw2[b, u], w2[WHOLE + u].rearrange("(p j) n -> p j n", j=PACK)[:, :, b * P : (b + 1) * P])
+                    raw2[b, u] = keep.tile([P, PACK * P], F32, name=f"raw2_{b}_{u}", align_bytes=64)[:]
+                nc.sync.dma_start(raw2[b, u].rearrange("p (j n) -> p j n", j=PACK), w2[WHOLE + u].rearrange("(p j) n -> p j n", j=PACK)[:, :, b * P : (b + 1) * P])
             nc.sync.dma_start(window[b][:, SLOTS : SLOTS + T], xr[b * P : (b + 1) * P, :])
-            if b == 0:
-                for r, pos in enumerate((pos1, pos2, pos3)):
-                    pos_sb.append(keep.tile([P, T // 16], U16, name=f"pos_sb{r}"))
-                    nc.sync.dma_start(pos_sb[r][:], pos)
 
         ident = keep.tile([P, P], F32, name="ident")
         make_identity(nc, ident[:])
@@ -85,17 +90,18 @@ def tile_moe_cpy_glu_gelu_kernel(tc, x_words, x_scales, xr, w1, w3, w2, gate, of
         slot_words = keep.tile([P, SLOTS], U32, name="slot_words", align_bytes=64)
         slot_scales = keep.tile([P, SLOTS], U8, name="slot_scales", align_bytes=64)
         half = SLOTS // 2
-        for a in range(2):
+
+        def fetch_tokens(slot_side, token_side, a):
             part = offs_sb[:, a * half // 16 : (a + 1) * half // 16]
-            nc.vector.tensor_copy(slot_words[:, a * half : (a + 1) * half], tok_words[:].indirect(part))
-            nc.vector.tensor_copy(slot_scales[:, a * half : (a + 1) * half], tok_scales[:].indirect(part))
+            nc.vector.tensor_copy(slot_side[:, a * half : (a + 1) * half], token_side[:].indirect(part))
 
         gates = keep.tile([P, TOP, T], F32, name="gates")
-        for r in range(TOP):
-            spread = held.tile([P, 4, P], F32, name="spread", tag=f"held{r}")
+
+        def spread_gate(r):
+            spread = bank(5 + r, T)
             for c in range(4):
-                nc.tensor.transpose(spread[:, c, :], gate_cols[:, r, c : c + 1].to_broadcast([P, P]), ident[:])
-            nc.scalar.copy(gates[:, r, :].rearrange("p (n c) -> p n c", c=4), spread[:].rearrange("p c n -> p n c"))
+                nc.tensor.transpose(spread[:, c * P : (c + 1) * P], gate_cols[:, r, c : c + 1].to_broadcast([P, P]), ident[:])
+            nc.scalar.copy(gates[:, r, :].rearrange("p (n c) -> p n c", c=4), spread[:].rearrange("p (c n) -> p n c", c=4))
 
         def interleave(copy, grouped, raw):
             copy(grouped.rearrange("p (c i) j -> p c j i", i=4), raw.rearrange("p j (c i) -> p c j i", i=4))
@@ -108,13 +114,12 @@ def tile_moe_cpy_glu_gelu_kernel(tc, x_words, x_scales, xr, w1, w3, w2, gate, of
         turned = {}
         acts = {}
 
-        def cast13(e, m):
+        def cast_whole(m, raw, split):
             grouped = stage[m][:].rearrange("p (c j) -> p c j", j=PACK)
-            if (e, m) == (E - 1, 1):
-                interleave(nc.scalar.copy, grouped[:, VEC_COLS:, :], raw13[e, m][:, :, VEC_COLS:])
-                interleave(nc.vector.tensor_copy, grouped[:, :VEC_COLS, :], raw13[e, m][:, :, :VEC_COLS])
-            else:
-                interleave((nc.vector.tensor_copy, nc.scalar.copy)[m], grouped, raw13[e, m][:])
+            if split > 0:
+                interleave(nc.vector.tensor_copy, grouped[:, :split, :], raw[:, :, :split])
+            if split < H:
+                interleave(nc.scalar.copy, grouped[:, split:, :], raw[:, :, split:])
 
         def codes(m):
             w_words = ring3.tile([P, H], U32, name="w_words", align_bytes=64)
@@ -125,7 +130,7 @@ def tile_moe_cpy_glu_gelu_kernel(tc, x_words, x_scales, xr, w1, w3, w2, gate, of
         def product13(e, m):
             slots = slice(e * C, (e + 1) * C)
             w_words, w_scales = codes(m)
-            sums[e, m] = acc.tile([P, H], F32, name="sums", tag="acc")
+            sums[e, m] = bank((2 * e + m) % 4, H)
             nc.tensor.matmul_mx(out=sums[e, m][:], lhsT=slot_words[:, slots].bitcast(FP8X4), lhsT_scale=slot_scales[:, slots],
                                 rhs=w_words[:].bitcast(FP8X4), rhs_scale=w_scales[:], start=True, stop=True)
 
@@ -135,21 +140,29 @@ def tile_moe_cpy_glu_gelu_kernel(tc, x_words, x_scales, xr, w1, w3, w2, gate, of
 
         def hidden_rows(e, pairs):
             nc.vector.tensor_tensor(pairs.bitcast(BF16), sums[e, 1][:], acts[e], MULT)
-            turned[e] = held.tile([P, 2, C], F32, name="turned", tag=f"held{2 + e % 2}")
+            turned[e] = bank(4 + e % 2, 2 * C)
             for u in range(2):
-                nc.tensor.transpose(turned[e][:, u, :], pairs[:, u : H // 2 : 2], ident[:])
+                nc.tensor.transpose(turned[e][:, u * C : (u + 1) * C], pairs[:, u : H // 2 : 2], ident[:])
 
         def hidden_codes(e, pairs):
             slots = slice(e * C, (e + 1) * C)
-            nc.scalar.copy(pairs.rearrange("p (s u) -> p s u", u=2), turned[e][:].rearrange("p u s -> p s u"))
+            nc.scalar.copy(pairs.rearrange("p (s u) -> p s u", u=2), turned[e][:].rearrange("p (u s) -> p s u", u=2))
             nc.vector.quantize_mx(out=h_words[:, slots].bitcast(FP8X4), scales=h_scales[:, slots], in_=pairs.bitcast(BF16))
 
+        for a in range(2):
+            fetch_tokens(slot_words, tok_words, a)
+        for r in range(TOP):
+            spread_gate(r)
         for e in range(E):
-            cast13(e, 0)
+            cast_whole(0, raw13[e, 0][:], VEC_13.get((e, 0), H))
+            if e == 0:
+                fetch_tokens(slot_scales, tok_scales, 0)
             if e > 0:
                 hidden_rows(e - 1, raw13[e, 0][:, 0, : H // 2])
             product13(e, 0)
-            cast13(e, 1)
+            cast_whole(1, raw13[e, 1][:], VEC_13.get((e, 1), 0))
+            if e == 0:
+                fetch_tokens(slot_scales, tok_scales, 1)
             product13(e, 1)
             if e > 0:
                 hidden_codes(e - 1, raw13[e, 1][:, 0, H // 2 :])
@@ -160,51 +173,59 @@ def tile_moe_cpy_glu_gelu_kernel(tc, x_words, x_scales, xr, w1, w3, w2, gate, of
             nc.tensor.matmul_mx(out=out_cols, lhsT=words[:, cols].bitcast(FP8X4), lhsT_scale=scales[:, cols],
                                 rhs=h_words[:, slots].bitcast(FP8X4), rhs_scale=h_scales[:, slots], start=True, stop=True)
 
-        early = [acc.tile([P, 2, WHOLE * C], F32, name="early", tag="acc") for i in range(2)]
+        whole_codes = []
         for e in range(WHOLE):
-            grouped = stage[e][:].rearrange("p (c j) -> p c j", j=PACK)
+            cast_whole(e, whole2[e][:], VEC_COLS[e])
             if e == 0:
-                interleave(nc.vector.tensor_copy, grouped, whole2[e][:])
                 hidden_rows(E - 1, whole2[e][:, 0, : H // 2])
             else:
-                interleave(nc.vector.tensor_copy, grouped[:, : K // 2, :], whole2[e][:, :, : K // 2])
-                interleave(nc.scalar.copy, grouped[:, K // 2 :, :], whole2[e][:, :, K // 2 :])
                 hidden_codes(E - 1, whole2[e][:, 0, K // 2 :])
-            w_words, w_scales = codes(e)
-            for b in range(BLOCKS):
-                second(early[b // 2][:, b % 2, e * C : (e + 1) * C], w_words, w_scales, slice(b * P, (b + 1) * P), e)
-
-        def empty_early(b):
-            nc.scalar.copy(window[b][:, : WHOLE * C], early[b // 2][:, b % 2, :])
+            whole_codes.append(codes(e))
 
         last = BLOCKS - 1
-        HALF = 2 * P * PACK
-        wide = {b: keep.tile([P, HALF + 3 * HALF // 4], BF16, name=f"wide{b}", align_bytes=64) for b in range(1, BLOCKS)}
-        alone = {key: keep.tile([P, HALF], BF16, name=f"alone{key[0]}{key[1]}", align_bytes=64)[:] for key in ((0, 0), (0, 1), (1, 0))}
+        PIECE = P * PACK
+        staged = {}
+        late = {}
 
-        def staged(b, a):
-            if (b, a) in alone:
-                return alone[b, a]
-            return wide[b][:, :HALF] if a == 1 else wide[b - 1][:, 3 * HALF // 4 :]
+        def shared(b, a, shape, dtype):
+            return keep.tile(shape, dtype, name="shared", tag=f"shared{b}_{a}", align_bytes=64)
 
-        def cast2(b):
-            nc.scalar.copy(staged(b, 0).rearrange("p (u c i j) -> p u c j i", u=2, i=4, j=PACK), raw2[b, "pair"].rearrange("p u j (c i) -> p u c j i", i=4))
-            for u in range(2):
-                interleave(nc.vector.tensor_copy if (b, u) == (0, 1) else nc.scalar.copy, staged(b, 1).rearrange("p (c j) -> p c j", j=PACK)[:, u * P : (u + 1) * P, :], raw2[b, 2 + u])
+        def cast2(b, u, copy):
+            if u % 2 == 0:
+                staged[b, u // 2] = shared(b, u // 2, [P, 2 * PIECE], BF16)
+            place = staged[b, u // 2][:, (u % 2) * PIECE : (u % 2 + 1) * PIECE]
+            interleave(copy, place.rearrange("p (c j) -> p c j", j=PACK), raw2[b, u].rearrange("p (j n) -> p j n", j=PACK))
 
-        def product2(b):
-            w2_words = ring2.tile([P, 4 * P], U32, name="w2_words", align_bytes=64)
-            w2_scales = ring2.tile([P, 4 * P], U8, name="w2_scales", align_bytes=64)
-            if b < last:
-                bank = acc.tile([P, 4 * C], F32, name="y_sums", tag="acc")
+        def product2(b, first, count, y):
+            a = first // 2
+            if first % 2 == 0:
+                if a == 0 or b == 0:
+                    late[b, a] = (ring2.tile([P, 2 * P], U32, name="late_words", align_bytes=64), ring2.tile([P, 2 * P], U8, name="late_scales", align_bytes=64))
+                else:
+                    late[b, a] = (shared(b + 1, 0, [P, 2 * P], U32), shared(b + 1, 1, [P, 2 * P], U8))
+            words, scales = late[b, a]
+            at = first % 2
+            cols = slice(at * P, (at + count) * P)
+            nc.vector.quantize_mx(out=words[:, cols].bitcast(FP8X4), scales=scales[:, cols], in_=staged[b, a][:, at * PIECE : (at + count) * PIECE])
+            for u in range(count):
+                second(y[:, u * C : (u + 1) * C], words, scales, slice((at + u) * P, (at + u + 1) * P), WHOLE + first + u)
+
+        def first_four(b):
+            y = bank(b % 2, 4 * C)
+            for e in range(WHOLE):
+                second(y[:, e * C : (e + 1) * C], *whole_codes[e], slice(b * P, (b + 1) * P), e)
+            product2(b, 0, 2, y[:, WHOLE * C :])
+            nc.scalar.copy(window[b][:, : 4 * C], y[:])
+
+        def last_two(b):
+            y = bank(2 + b % 2, 2 * C)
+            if b == 0:
+                product2(b, 2, 1, y[:, :C])
+                product2(b, 3, 1, y[:, C:])
+                nc.vector.tensor_copy(window[b][:, 4 * C : SLOTS], y[:])
             else:
-                bank = held.tile([P, 4 * C], F32, name="y_last", tag="held3")
-            for a in range(2):
-                cols = slice(2 * a * P, 2 * (a + 1) * P)
-                nc.vector.quantize_mx(out=w2_words[:, cols].bitcast(FP8X4), scales=w2_scales[:, cols], in_=staged(b, a))
-                for u in range(2 * a, 2 * a + 2):
-                    second(bank[:, u * C : (u + 1) * C], w2_words, w2_scales, slice(u * P, (u + 1) * P), WHOLE + u)
-            (nc.vector.tensor_copy if b == 0 else nc.scalar.copy)(window[b][:, WHOLE * C : SLOTS], bank[:])
+                product2(b, 2, 2, y)
+                nc.scalar.copy(window[b][:, 4 * C : SLOTS], y[:])
 
         picked = {}
         summed = {}
@@ -214,70 +235,78 @@ def tile_moe_cpy_glu_gelu_kernel(tc, x_words, x_scales, xr, w1, w3, w2, gate, of
             offsets = pos_sb[r][:, cols.start // 16 : cols.stop // 16]
             nc.vector.tensor_tensor(picked[b, r][:, cols], window[b][:].indirect(offsets), gates[:, r, cols], MULT)
 
-        def add_turned(b):
-            if b < 2:
-                bank = held.tile([P, T // P, P], F32, name="summed", tag=f"held{b}")
-                summed[b] = [bank[:, c, :] for c in range(T // P)]
-                summed[b, "bank"] = bank[:].rearrange("p c n -> p (c n)")
-            else:
-                summed[b] = [acc.tile([P, P], F32, name="summed_part", tag="acc")[:] for c in range(T // P)]
-            for c in reversed(range(T // P)):
+        def add_pass(b, c, r):
+            nc.tensor.matmul(summed[b][c], lhsT=picked[b, r][:, c * P : (c + 1) * P], rhs=ident[:], is_transpose=True, start=r == 0, stop=r == TOP - 1)
+
+        def add_in_one_bank(b, i):
+            whole = bank(i, T)
+            summed[b] = [whole[:, c * P : (c + 1) * P] for c in range(T // P)]
+            summed[b, "bank"] = whole[:]
+            for c in range(T // P):
                 for r in range(TOP):
-                    nc.tensor.matmul(summed[b][c], lhsT=picked[b, r][:, c * P : (c + 1) * P], rhs=ident[:], is_transpose=True, start=r == 0, stop=r == TOP - 1)
+                    add_pass(b, c, r)
+
+        def add_in_banks(b, banks):
+            summed[b] = [bank(i, P)[:] for i in banks]
+            for r in range(TOP):
+                for c in range(len(banks)):
+                    add_pass(b, c, r)
 
         def empty_turned(b, place):
             summed_sb[b] = place
-            if b < 2:
+            if (b, "bank") in summed:
                 nc.scalar.copy(place, summed[b, "bank"])
             else:
-                for c in reversed(range(T // P)):
+                for c in range(len(summed[b])):
                     nc.scalar.copy(place[:, c * P : (c + 1) * P], summed[b][c])
 
-        def turn_back(b, tag):
-            back = held.tile([P, T], F32, name="back", tag=tag)
-            for c in range(T // P):
+        def turn_back(b, i, total):
+            width = len(summed[b]) * P
+            back = bank(i, width)
+            for c in range(len(summed[b])):
                 nc.tensor.transpose(back[:, c * P : (c + 1) * P], summed_sb[b][:, c * P : (c + 1) * P], ident[:])
-            total = raw13[b, 0][:, 1, :]
             nc.scalar.copy(total, back[:])
-            nc.scalar.dma_start(out[b * P : (b + 1) * P, :], total)
+            nc.sync.dma_start(out[b * P : (b + 1) * P, :width], total)
 
         left, right = slice(0, T // 2), slice(T // 2, T)
-        cast2(0)
-        empty_early(0)
-        product2(0)
-        for b in range(BLOCKS):
+        for u in range(CUT):
+            cast2(0, u, nc.vector.tensor_copy if u == CUT - 1 else nc.scalar.copy)
+            if u == 1:
+                first_four(0)
+        last_two(0)
+        for b in range(last):
             picked[b, 0] = ring2.tile([P, T], F32, name="picked0")[:]
-            picked[b, 1] = ring2.tile([P, T], F32, name="picked1")[:]
             fetch(b, 0)
+            for u in range(CUT):
+                cast2(b + 1, u, nc.scalar.copy)
+                if (b + 1, u) == (last, 1):
+                    turn_back(0, 2, raw2[last, 1])
+            first_four(b + 1)
+            if b > 0:
+                empty_turned(b - 1, raw2[b + 1, CUT - 2])
+            picked[b, 1] = shared(b + 1, 0, [P, T], F32)[:]
             fetch(b, 1)
-            if b == last:
-                break
-            cast2(b + 1)
-            if b == 0:
-                empty_early(1)
-                empty_early(2)
-            else:
-                if b == 1:
-                    empty_early(3)
-                empty_turned(b - 1, raw2[b + 1, 3].rearrange("p j n -> p (j n)"))
-            product2(b + 1)
-            picked[b, 2] = staged(b + 1, 1).bitcast(F32)
+            last_two(b + 1)
+            picked[b, 2] = shared(b + 1, 1, [P, T], F32)[:]
+            fetch(b, 2)
             if b < 2:
-                fetch(b, 2, right)
-                fetch(b, 2, left)
+                add_in_one_bank(b, 4 + b)
             else:
-                fetch(b, 2)
-            add_turned(b)
-        turn_back(0, "held3")
+                add_in_banks(b, (6, 7, 4, 0))
+        turn_back(1, 3, raw13[1, 0][:, 1, :])
         empty_turned(2, raw13[2, 0][:, 2, :])
-        turn_back(1, "held3")
-        turn_back(2, "held0")
-        picked[last, 2] = raw13[last, 0][:, 3, :]
-        two = raw13[last, 0][:, 2, :]
-        total = raw13[last, 0][:, 1, :]
-        fetch(last, 2, left)
-        nc.vector.tensor_tensor(two, picked[last, 0], picked[last, 1], ADD)
-        fetch(last, 2, right)
-        for cols in (left, right):
-            nc.vector.tensor_tensor(total[:, cols], two[:, cols], picked[last, 2][:, cols], ADD)
-            nc.sync.dma_start(out[last * P :, cols], total[:, cols])
+        turn_back(2, 5, raw13[2, 0][:, 1, :])
+        for r in range(TOP):
+            picked[last, r] = raw13[last, 1][:, r, :]
+        for r in range(TOP):
+            fetch(last, r, left)
+        add_in_banks(last, (1, 2))
+        empty_turned(last, raw13[last, 0][:, 3, left])
+        turn_back(last, 6, raw13[last, 0][:, 1, left])
+        for r in range(TOP):
+            fetch(last, r, right)
+        two = raw13[last, 0][:, 2, right]
+        total = raw13[last, 0][:, 1, right]
+        nc.vector.tensor_tensor(two, picked[last, 0][:, right], picked[last, 1][:, right], ADD)
+        nc.vector.tensor_tensor(total, two, picked[last, 2][:, right], ADD)
+        nc.sync.dma_start(out[last * P :, right], total)

@@ -266,7 +266,7 @@ def tile_moe_cpy_glu_gelu_kernel(tc, x_words, x_scales, xr, w1, w3, w2, gate, of
             for c in range(len(summed[b])):
                 nc.tensor.transpose(back[:, c * P : (c + 1) * P], summed_sb[b][:, c * P : (c + 1) * P], ident[:])
             nc.scalar.copy(total, back[:])
-            nc.sync.dma_start(out[b * P : (b + 1) * P, :width], total)
+            (nc.scalar if b >= 2 else nc.sync).dma_start(out[b * P : (b + 1) * P, :width], total)
 
         left, right = slice(0, T // 2), slice(T // 2, T)
         for u in range(CUT):
@@ -282,8 +282,8 @@ def tile_moe_cpy_glu_gelu_kernel(tc, x_words, x_scales, xr, w1, w3, w2, gate, of
                 if (b + 1, u) == (last, 1):
                     turn_back(0, 2, raw2[last, 1])
             first_four(b + 1)
-            if b > 0:
-                empty_turned(b - 1, raw2[b + 1, CUT - 2])
+            if b == 1:
+                empty_turned(0, raw2[2, CUT - 2])
             picked[b, 1] = shared(b + 1, 0, [P, T], F32)[:]
             fetch(b, 1)
             last_two(b + 1)
@@ -293,15 +293,16 @@ def tile_moe_cpy_glu_gelu_kernel(tc, x_words, x_scales, xr, w1, w3, w2, gate, of
                 add_in_one_bank(b, 4 + b)
             else:
                 add_in_banks(b, (6, 7, 4, 0))
-        turn_back(1, 3, raw13[1, 0][:, 1, :])
+        empty_turned(1, shared(BLOCKS, 0, [P, T], F32)[:])
         empty_turned(2, raw13[2, 0][:, 2, :])
-        turn_back(2, 5, raw13[2, 0][:, 1, :])
+        turn_back(1, 3, raw13[1, 0][:, 1, :])
         for r in range(TOP):
             picked[last, r] = raw13[last, 1][:, r, :]
         for r in range(TOP):
             fetch(last, r, left)
         add_in_banks(last, (1, 2))
         empty_turned(last, raw13[last, 0][:, 3, left])
+        turn_back(2, 5, raw13[2, 0][:, 1, :])
         turn_back(last, 6, raw13[last, 0][:, 1, left])
         for r in range(TOP):
             fetch(last, r, right)

@@ -22,10 +22,12 @@ GELU = mybir.ActivationFunctionType.Gelu_apprx_tanh
 P = 128
 PACK = 4
 BLOCKS = K // P
+LAST = BLOCKS - 1
 WHOLE = 2
 CUT = E - WHOLE
-VEC_COLS = (336, 336)
-VEC_13 = {(E - 2, 1): 144, (E - 1, 0): 336, (E - 1, 1): 256}
+PIECE = P * PACK
+VEC_BOTH_FREE = 336
+VEC_13 = {(E - 2, 1): 144, (E - 1, 0): VEC_BOTH_FREE, (E - 1, 1): 256}
 
 
 def tile_moe_cpy_glu_gelu_kernel(tc, x_words, x_scales, xr, w1, w3, w2, gate, offs, pos1, pos2, pos3, out):
@@ -57,21 +59,16 @@ def tile_moe_cpy_glu_gelu_kernel(tc, x_words, x_scales, xr, w1, w3, w2, gate, of
         for q in range(4):
             nc.sync.dma_start(tok_scales[32 * q : 32 * q + 4, :].bitcast(I32), x_scales[0, 4 * q : 4 * q + 4, :].bitcast(I32))
         load13(0, 1)
-        load13(1, 0)
-        load13(1, 1)
-        pos_sb = []
-        for e in range(2, E):
+        for e in range(1, E):
             load13(e, 0)
             load13(e, 1)
-            if e - 2 < TOP:
-                pos_sb.append(keep.tile([P, T // 16], U16, name=f"pos_sb{e - 2}"))
-                nc.sync.dma_start(pos_sb[e - 2][:], (pos1, pos2, pos3)[e - 2])
         whole2 = []
         for e in range(WHOLE):
             whole2.append(keep.tile([P, PACK, K], F32, name=f"whole2_{e}", align_bytes=64))
             nc.sync.dma_start(whole2[e][:], w2[e].rearrange("(p j) n -> p j n", j=PACK))
         raw2 = {}
         window = []
+        pos_sb = []
         for b in range(BLOCKS):
             window.append(keep.tile([P, WIN], F32, name=f"window{b}", align_bytes=64))
             nc.gpsimd.memset(window[b][:, SLOTS + T :], 0.0)
@@ -83,6 +80,10 @@ def tile_moe_cpy_glu_gelu_kernel(tc, x_words, x_scales, xr, w1, w3, w2, gate, of
                     raw2[b, u] = keep.tile([P, PACK * P], F32, name=f"raw2_{b}_{u}", align_bytes=64)[:]
                 nc.sync.dma_start(raw2[b, u].rearrange("p (j n) -> p j n", j=PACK), w2[WHOLE + u].rearrange("(p j) n -> p j n", j=PACK)[:, :, b * P : (b + 1) * P])
             nc.sync.dma_start(window[b][:, SLOTS : SLOTS + T], xr[b * P : (b + 1) * P, :])
+            if b == 0:
+                for r, pos in enumerate((pos1, pos2, pos3)):
+                    pos_sb.append(keep.tile([P, T // 16], U16, name=f"pos_sb{r}"))
+                    nc.sync.dma_start(pos_sb[r][:], pos)
 
         ident = keep.tile([P, P], F32, name="ident")
         make_identity(nc, ident[:])
@@ -175,15 +176,13 @@ def tile_moe_cpy_glu_gelu_kernel(tc, x_words, x_scales, xr, w1, w3, w2, gate, of
 
         whole_codes = []
         for e in range(WHOLE):
-            cast_whole(e, whole2[e][:], VEC_COLS[e])
+            cast_whole(e, whole2[e][:], VEC_BOTH_FREE)
             if e == 0:
                 hidden_rows(E - 1, whole2[e][:, 0, : H // 2])
             else:
                 hidden_codes(E - 1, whole2[e][:, 0, K // 2 :])
             whole_codes.append(codes(e))
 
-        last = BLOCKS - 1
-        PIECE = P * PACK
         staged = {}
         late = {}
 
@@ -229,6 +228,7 @@ def tile_moe_cpy_glu_gelu_kernel(tc, x_words, x_scales, xr, w1, w3, w2, gate, of
 
         picked = {}
         summed = {}
+        one_bank = {}
         summed_sb = {}
 
         def fetch(b, r, cols=slice(0, T)):
@@ -241,7 +241,7 @@ def tile_moe_cpy_glu_gelu_kernel(tc, x_words, x_scales, xr, w1, w3, w2, gate, of
         def add_in_one_bank(b, i):
             whole = bank(i, T)
             summed[b] = [whole[:, c * P : (c + 1) * P] for c in range(T // P)]
-            summed[b, "bank"] = whole[:]
+            one_bank[b] = whole[:]
             for c in range(T // P):
                 for r in range(TOP):
                     add_pass(b, c, r)
@@ -254,8 +254,8 @@ def tile_moe_cpy_glu_gelu_kernel(tc, x_words, x_scales, xr, w1, w3, w2, gate, of
 
         def empty_turned(b, place):
             summed_sb[b] = place
-            if (b, "bank") in summed:
-                nc.scalar.copy(place, summed[b, "bank"])
+            if b in one_bank:
+                nc.scalar.copy(place, one_bank[b])
             else:
                 for c in range(len(summed[b])):
                     nc.scalar.copy(place[:, c * P : (c + 1) * P], summed[b][c])
@@ -266,7 +266,7 @@ def tile_moe_cpy_glu_gelu_kernel(tc, x_words, x_scales, xr, w1, w3, w2, gate, of
             for c in range(len(summed[b])):
                 nc.tensor.transpose(back[:, c * P : (c + 1) * P], summed_sb[b][:, c * P : (c + 1) * P], ident[:])
             nc.scalar.copy(total, back[:])
-            (nc.scalar if b >= 2 else nc.sync).dma_start(out[b * P : (b + 1) * P, :width], total)
+            (nc.scalar if b >= LAST - 1 else nc.sync).dma_start(out[b * P : (b + 1) * P, :width], total)
 
         left, right = slice(0, T // 2), slice(T // 2, T)
         for u in range(CUT):
@@ -274,13 +274,13 @@ def tile_moe_cpy_glu_gelu_kernel(tc, x_words, x_scales, xr, w1, w3, w2, gate, of
             if u == 1:
                 first_four(0)
         last_two(0)
-        for b in range(last):
+        for b in range(LAST):
             picked[b, 0] = ring2.tile([P, T], F32, name="picked0")[:]
             fetch(b, 0)
             for u in range(CUT):
                 cast2(b + 1, u, nc.scalar.copy)
-                if (b + 1, u) == (last, 1):
-                    turn_back(0, 2, raw2[last, 1])
+                if (b + 1, u) == (LAST, 1):
+                    turn_back(0, 2, raw2[LAST, 1])
             first_four(b + 1)
             if b == 1:
                 empty_turned(0, raw2[2, CUT - 2])
@@ -289,7 +289,7 @@ def tile_moe_cpy_glu_gelu_kernel(tc, x_words, x_scales, xr, w1, w3, w2, gate, of
             last_two(b + 1)
             picked[b, 2] = shared(b + 1, 1, [P, T], F32)[:]
             fetch(b, 2)
-            if b < 2:
+            if b < LAST - 1:
                 add_in_one_bank(b, 4 + b)
             else:
                 add_in_banks(b, (6, 7, 4, 0))
@@ -297,17 +297,17 @@ def tile_moe_cpy_glu_gelu_kernel(tc, x_words, x_scales, xr, w1, w3, w2, gate, of
         empty_turned(2, raw13[2, 0][:, 2, :])
         turn_back(1, 3, raw13[1, 0][:, 1, :])
         for r in range(TOP):
-            picked[last, r] = raw13[last, 1][:, r, :]
+            picked[LAST, r] = raw13[LAST, 1][:, r, :]
         for r in range(TOP):
-            fetch(last, r, left)
-        add_in_banks(last, (1, 2))
-        empty_turned(last, raw13[last, 0][:, 3, left])
+            fetch(LAST, r, left)
+        add_in_banks(LAST, (1, 2))
+        empty_turned(LAST, raw13[LAST, 0][:, 3, left])
         turn_back(2, 5, raw13[2, 0][:, 1, :])
-        turn_back(last, 6, raw13[last, 0][:, 1, left])
+        turn_back(LAST, 6, raw13[LAST, 0][:, 1, left])
         for r in range(TOP):
-            fetch(last, r, right)
-        two = raw13[last, 0][:, 2, right]
-        total = raw13[last, 0][:, 1, right]
-        nc.vector.tensor_tensor(two, picked[last, 0][:, right], picked[last, 1][:, right], ADD)
-        nc.vector.tensor_tensor(total, two, picked[last, 2][:, right], ADD)
-        nc.sync.dma_start(out[last * P :, right], total)
+            fetch(LAST, r, right)
+        two = raw13[LAST, 0][:, 2, right]
+        total = raw13[LAST, 0][:, 1, right]
+        nc.vector.tensor_tensor(two, picked[LAST, 0][:, right], picked[LAST, 1][:, right], ADD)
+        nc.vector.tensor_tensor(total, two, picked[LAST, 2][:, right], ADD)
+        nc.sync.dma_start(out[LAST * P :, right], total)

@@ -25,9 +25,11 @@ BLOCKS = K // P
 LAST = BLOCKS - 1
 WHOLE = 2
 CUT = E - WHOLE
+RUN = 16
 PIECE = P * PACK
 VEC_BOTH_FREE = 336
-VEC_13 = {(E - 2, 1): 144, (E - 1, 0): VEC_BOTH_FREE, (E - 1, 1): 256}
+VEC_LATE = 256
+VEC_13 = {(E - 2, 1): 144, (E - 1, 0): VEC_BOTH_FREE, (E - 1, 1): VEC_LATE}
 
 
 def tile_moe_cpy_glu_gelu_kernel(tc, x_words, x_scales, xr, w1, w3, w2, gate, offs, pos1, pos2, pos3, out):
@@ -54,8 +56,10 @@ def tile_moe_cpy_glu_gelu_kernel(tc, x_words, x_scales, xr, w1, w3, w2, gate, of
         tok_words = keep.tile([P, T], U32, name="tok_words", align_bytes=64)
         nc.sync.dma_start(tok_words[:].bitcast(I32), x_words[0].rearrange("p t d -> p (t d)").bitcast(I32))
         load13(0, 0)
-        gate_cols = keep.tile([P, TOP, 4], F32, name="gate_cols")
-        nc.sync.dma_start(gate_cols[:], gate[:, 0, :].rearrange("r (p c) -> p r c", c=4))
+        runs = TOP * T // RUN
+        gate_cols = keep.tile([P, RUN], F32, name="gate_cols")
+        nc.sync.dma_start(gate_cols[:runs, :], gate.rearrange("r q (a c) -> (r q a) c", c=RUN)[0 : (runs - 1) * (P + 1) + 1 : P + 1, :])
+        nc.gpsimd.memset(gate_cols[runs:, :], 0.0)
         for q in range(4):
             nc.sync.dma_start(tok_scales[32 * q : 32 * q + 4, :].bitcast(I32), x_scales[0, 4 * q : 4 * q + 4, :].bitcast(I32))
         load13(0, 1)
@@ -98,11 +102,12 @@ def tile_moe_cpy_glu_gelu_kernel(tc, x_words, x_scales, xr, w1, w3, w2, gate, of
 
         gates = keep.tile([P, TOP, T], F32, name="gates")
 
-        def spread_gate(r):
-            spread = bank(5 + r, T)
+        def spread_gate(a):
+            spread = bank(4 + a, 4 * P)
             for c in range(4):
-                nc.tensor.transpose(spread[:, c * P : (c + 1) * P], gate_cols[:, r, c : c + 1].to_broadcast([P, P]), ident[:])
-            nc.scalar.copy(gates[:, r, :].rearrange("p (n c) -> p n c", c=4), spread[:].rearrange("p (c n) -> p n c", c=4))
+                nc.tensor.transpose(spread[:, c * P : (c + 1) * P], gate_cols[:, 4 * a + c : 4 * a + c + 1].to_broadcast([P, P]), ident[:])
+            by_run = gates[:].rearrange("p r (n c) -> p (r n) c", c=RUN)
+            nc.scalar.copy(by_run[:, :, 4 * a : 4 * a + 4], spread[:].rearrange("p (c n) -> p n c", c=4)[:, :runs, :])
 
         def interleave(copy, grouped, raw):
             copy(grouped.rearrange("p (c i) j -> p c j i", i=4), raw.rearrange("p j (c i) -> p c j i", i=4))
@@ -152,8 +157,8 @@ def tile_moe_cpy_glu_gelu_kernel(tc, x_words, x_scales, xr, w1, w3, w2, gate, of
 
         for a in range(2):
             fetch_tokens(slot_words, tok_words, a)
-        for r in range(TOP):
-            spread_gate(r)
+        for a in range(RUN // 4):
+            spread_gate(a)
         for e in range(E):
             cast_whole(0, raw13[e, 0][:], VEC_13.get((e, 0), H))
             if e == 0:
@@ -176,7 +181,7 @@ def tile_moe_cpy_glu_gelu_kernel(tc, x_words, x_scales, xr, w1, w3, w2, gate, of
 
         whole_codes = []
         for e in range(WHOLE):
-            cast_whole(e, whole2[e][:], VEC_BOTH_FREE)
+            cast_whole(e, whole2[e][:], VEC_LATE)
             if e == 0:
                 hidden_rows(E - 1, whole2[e][:, 0, : H // 2])
             else:

@@ -71,6 +71,7 @@ def tile_moe_cpy_glu_gelu_kernel(tc, x_words, x_scales, xr, w1, w3, w2, gate, of
             whole2.append(keep.tile([P, PACK, K], F32, name=f"whole2_{e}", align_bytes=64))
             nc.sync.dma_start(whole2[e][:], w2[e].rearrange("(p j) n -> p j n", j=PACK))
         raw2 = {}
+        wide = {}
         window = []
         pos_sb = []
         for b in range(BLOCKS):
@@ -78,8 +79,11 @@ def tile_moe_cpy_glu_gelu_kernel(tc, x_words, x_scales, xr, w1, w3, w2, gate, of
             nc.gpsimd.memset(window[b][:, SLOTS + T :], 0.0)
         for b in range(BLOCKS):
             for u in range(CUT):
-                if b > 0 and u == CUT - 1:
+                if b > 0 and u == CUT - 2:
                     raw2[b, u] = window[b][:, : PACK * P]
+                elif b > 0 and u == CUT - 1:
+                    wide[b] = keep.tile([P, 2 * T], F32, name=f"wide{b}", align_bytes=64)
+                    raw2[b, u] = wide[b][:, T // 2 : T // 2 + PACK * P]
                 else:
                     raw2[b, u] = keep.tile([P, PACK * P], F32, name=f"raw2_{b}_{u}", align_bytes=64)[:]
                 nc.sync.dma_start(raw2[b, u].rearrange("p (j n) -> p j n", j=PACK), w2[WHOLE + u].rearrange("(p j) n -> p j n", j=PACK)[:, :, b * P : (b + 1) * P])
@@ -203,7 +207,7 @@ def tile_moe_cpy_glu_gelu_kernel(tc, x_words, x_scales, xr, w1, w3, w2, gate, of
         def product2(b, first, count, y):
             a = first // 2
             if first % 2 == 0:
-                if a == 0 or b == 0:
+                if a == 0:
                     late[b, a] = (ring2.tile([P, 2 * P], U32, name="late_words", align_bytes=64), ring2.tile([P, 2 * P], U8, name="late_scales", align_bytes=64))
                 else:
                     late[b, a] = (shared(b + 1, 0, [P, 2 * P], U32), shared(b + 1, 1, [P, 2 * P], U8))
@@ -284,15 +288,15 @@ def tile_moe_cpy_glu_gelu_kernel(tc, x_words, x_scales, xr, w1, w3, w2, gate, of
             fetch(b, 0)
             for u in range(CUT):
                 cast2(b + 1, u, nc.scalar.copy)
-                if (b + 1, u) == (LAST, 1):
-                    turn_back(0, 2, raw2[LAST, 1])
             first_four(b + 1)
             if b == 1:
-                empty_turned(0, raw2[2, CUT - 2])
-            picked[b, 1] = shared(b + 1, 0, [P, T], F32)[:]
+                empty_turned(0, wide[2][:, T:])
+            if b == 2:
+                turn_back(0, 2, wide[LAST][:, T:])
+            picked[b, 1] = raw2[b + 1, 1]
             fetch(b, 1)
             last_two(b + 1)
-            picked[b, 2] = shared(b + 1, 1, [P, T], F32)[:]
+            picked[b, 2] = wide[b + 1][:, :T]
             fetch(b, 2)
             if b < LAST - 1:
                 add_in_one_bank(b, 4 + b)

@@ -49,6 +49,10 @@ def tile_moe_cpy_glu_gelu_kernel(tc, x_words, x_scales, xr, w1, w3, w2, gate, of
             raw13[e, m] = keep.tile([P, PACK, H], F32, name=f"raw13_{e}_{m}", align_bytes=64)
             nc.sync.dma_start(raw13[e, m][:], (w1, w3)[m][e].rearrange("(p j) c -> p j c", j=PACK))
 
+        warm = keep.tile([P, 2], F32, name="warm")
+        nc.vector.memset(warm[:, :1], 0.0)
+        nc.scalar.activation(warm[:, 1:], warm[:, :1], GELU)
+
         tok_scales = keep.tile([P, T], U8, name="tok_scales", align_bytes=64)
         nc.gpsimd.memset(tok_scales[:].bitcast(I32), 0)
         offs_sb = keep.tile([P, SLOTS // 16], U16, name="offs_sb")
@@ -226,12 +230,14 @@ def tile_moe_cpy_glu_gelu_kernel(tc, x_words, x_scales, xr, w1, w3, w2, gate, of
             nc.scalar.copy(window[b][:, : 4 * C], y[:])
 
         def last_two(b):
-            y = bank(2 + b % 2, 2 * C)
-            if b == 0:
-                product2(b, 2, 1, y[:, :C])
-                product2(b, 3, 1, y[:, C:])
-                nc.vector.tensor_copy(window[b][:, 4 * C : SLOTS], y[:])
+            if b < LAST:
+                for u in (2, 3):
+                    y = bank(u, C)
+                    product2(b, u, 1, y)
+                    copy = nc.vector.tensor_copy if (b, u) == (0, 3) else nc.scalar.copy
+                    copy(window[b][:, (WHOLE + u) * C : (WHOLE + u + 1) * C], y[:])
             else:
+                y = bank(2 + b % 2, 2 * C)
                 product2(b, 2, 2, y)
                 nc.scalar.copy(window[b][:, 4 * C : SLOTS], y[:])
 

@@ -49,10 +49,6 @@ def tile_moe_cpy_glu_gelu_kernel(tc, x_words, x_scales, xr, w1, w3, w2, gate, of
             raw13[e, m] = keep.tile([P, PACK, H], F32, name=f"raw13_{e}_{m}", align_bytes=64)
             nc.sync.dma_start(raw13[e, m][:], (w1, w3)[m][e].rearrange("(p j) c -> p j c", j=PACK))
 
-        warm = keep.tile([P, 2], F32, name="warm")
-        nc.vector.memset(warm[:, :1], 0.0)
-        nc.scalar.activation(warm[:, 1:], warm[:, :1], GELU)
-
         tok_scales = keep.tile([P, T], U8, name="tok_scales", align_bytes=64)
         nc.gpsimd.memset(tok_scales[:].bitcast(I32), 0)
         offs_sb = keep.tile([P, SLOTS // 16], U16, name="offs_sb")

from contextlib import ExitStack

import concourse.mybir as mybir
from concourse.masks import make_identity

K, T, E, C, H, TOP, PAD = 512, 512, 6, 128, 512, 3, 64
SLOTS = E * C
WIN = SLOTS + T + PAD
FLOPS = 2 * 3 * SLOTS * K * H

F32 = mybir.dt.float32
BF16 = mybir.dt.bfloat16
I32 = mybir.dt.int32
U32 = mybir.dt.uint32
U16 = mybir.dt.uint16
U8 = mybir.dt.uint8
FP8X4 = mybir.dt.float8_e4m3fn_x4
MULT = mybir.AluOpType.mult
ADD = mybir.AluOpType.add
GELU = mybir.ActivationFunctionType.Gelu_apprx_tanh

P = 128
PACK = 4
BLOCKS = K // P
LAST = BLOCKS - 1
WHOLE = 2
CUT = E - WHOLE
RUN = 16
PIECE = P * PACK
VEC_BOTH_FREE = 336
VEC_LATE = 256
VEC_13 = {(E - 2, 1): 144, (E - 1, 0): VEC_BOTH_FREE, (E - 1, 1): VEC_LATE}


def tile_moe_cpy_glu_gelu_kernel(tc, x_words, x_scales, xr, w1, w3, w2, gate, offs, pos1, pos2, pos3, out):
    nc = tc.nc
    with ExitStack() as ctx:
        keep = ctx.enter_context(tc.tile_pool(name="keep", bufs=1))
        ring3 = ctx.enter_context(tc.tile_pool(name="ring3", bufs=3))
        ring2 = ctx.enter_context(tc.tile_pool(name="ring2", bufs=2))
        psum = ctx.enter_context(tc.psum_pool(name="psum", bufs=1))

        def bank(i, cols):
            return psum.tile([P, cols], F32, name="bank", tag=f"bank{i}")

        raw13 = {}

        def load13(e, m):
            raw13[e, m] = keep.tile([P, PACK, H], F32, name=f"raw13_{e}_{m}", align_bytes=64)
            nc.sync.dma_start(raw13[e, m][:], (w1, w3)[m][e].rearrange("(p j) c -> p j c", j=PACK))

        tok_scales = keep.tile([P, T], U8, name="tok_scales", align_bytes=64)
        nc.gpsimd.memset(tok_scales[:].bitcast(I32), 0)
        offs_sb = keep.tile([P, SLOTS // 16], U16, name="offs_sb")
        nc.sync.dma_start(offs_sb[:], offs)
        tok_words = keep.tile([P, T], U32, name="tok_words", align_bytes=64)
        nc.sync.dma_start(tok_words[:].bitcast(I32), x_words[0].rearrange("p t d -> p (t d)").bitcast(I32))
        load13(0, 0)
        runs = TOP * T // RUN
        gate_cols = keep.tile([P, RUN], F32, name="gate_cols")
        nc.sync.dma_start(gate_cols[:runs, :], gate.rearrange("r q (a c) -> (r q a) c", c=RUN)[0 : (runs - 1) * (P + 1) + 1 : P + 1, :])
        nc.gpsimd.memset(gate_cols[runs:, :], 0.0)
        for q in range(4):
            nc.sync.dma_start(tok_scales[32 * q : 32 * q + 4, :].bitcast(I32), x_scales[0, 4 * q : 4 * q + 4, :].bitcast(I32))
        load13(0, 1)
        for e in range(1, E):
            load13(e, 0)
            load13(e, 1)
        whole2 = []
        for e in range(WHOLE):
            whole2.append(keep.tile([P, PACK, K], F32, name=f"whole2_{e}", align_bytes=64))
            nc.sync.dma_start(whole2[e][:], w2[e].rearrange("(p j) n -> p j n", j=PACK))
        raw2 = {}
        wide = {}
        window = []
        pos_sb = []
        for b in range(BLOCKS):
            window.append(keep.tile([P, WIN], F32, name=f"window{b}", align_bytes=64))
            nc.gpsimd.memset(window[b][:, SLOTS + T :], 0.0)
        for b in range(BLOCKS):
            for u in range(CUT):
                if b > 0 and u == CUT - 2:
                    raw2[b, u] = window[b][:, : PACK * P]
                elif b > 0 and u == CUT - 1:
                    wide[b] = keep.tile([P, 2 * T], F32, name=f"wide{b}", align_bytes=64)
                    raw2[b, u] = wide[b][:, T // 2 : T // 2 + PACK * P]
                else:
                    raw2[b, u] = keep.tile([P, PACK * P], F32, name=f"raw2_{b}_{u}", align_bytes=64)[:]
                nc.sync.dma_start(raw2[b, u].rearrange("p (j n) -> p j n", j=PACK), w2[WHOLE + u].rearrange("(p j) n -> p j n", j=PACK)[:, :, b * P : (b + 1) * P])
            nc.sync.dma_start(window[b][:, SLOTS : SLOTS + T], xr[b * P : (b + 1) * P, :])
            if b == 0:
                for r, pos in enumerate((pos1, pos2, pos3)):
                    pos_sb.append(keep.tile([P, T // 16], U16, name=f"pos_sb{r}"))
                    nc.sync.dma_start(pos_sb[r][:], pos)

        ident = keep.tile([P, P], F32, name="ident")
        make_identity(nc, ident[:])

        slot_words = keep.tile([P, SLOTS], U32, name="slot_words", align_bytes=64)
        slot_scales = keep.tile([P, SLOTS], U8, name="slot_scales", align_bytes=64)
        half = SLOTS // 2

        def fetch_tokens(slot_side, token_side, a):
            part = offs_sb[:, a * half // 16 : (a + 1) * half // 16]
            nc.vector.tensor_copy(slot_side[:, a * half : (a + 1) * half], token_side[:].indirect(part))

        gates = keep.tile([P, TOP, T], F32, name="gates")

        def spread_gate(a):
            spread = bank(4 + a, 4 * P)
            for c in range(4):
                nc.tensor.transpose(spread[:, c * P : (c + 1) * P], gate_cols[:, 4 * a + c : 4 * a + c + 1].to_broadcast([P, P]), ident[:])
            by_run = gates[:].rearrange("p r (n c) -> p (r n) c", c=RUN)
            nc.scalar.copy(by_run[:, :, 4 * a : 4 * a + 4], spread[:].rearrange("p (c n) -> p n c", c=4)[:, :runs, :])

        def interleave(copy, grouped, raw):
            copy(grouped.rearrange("p (c i) j -> p c j i", i=4), raw.rearrange("p j (c i) -> p c j i", i=4))

        h_words = keep.tile([P, SLOTS], U32, name="h_words", align_bytes=64)
        h_scales = keep.tile([P, SLOTS], U8, name="h_scales", align_bytes=64)

        stage = [keep.tile([P, H * PACK], BF16, name=f"stage{i}", align_bytes=64) for i in range(2)]
        sums = {}
        turned = {}
        acts = {}

        def cast_whole(m, raw, split):
            grouped = stage[m][:].rearrange("p (c j) -> p c j", j=PACK)
            if split > 0:
                interleave(nc.vector.tensor_copy, grouped[:, :split, :], raw[:, :, :split])
            if split < H:
                interleave(nc.scalar.copy, grouped[:, split:, :], raw[:, :, split:])

        def codes(m):
            w_words = ring3.tile([P, H], U32, name="w_words", align_bytes=64)
            w_scales = ring3.tile([P, H], U8, name="w_scales", align_bytes=64)
            nc.vector.quantize_mx(out=w_words[:].bitcast(FP8X4), scales=w_scales[:], in_=stage[m][:])
            return w_words, w_scales

        def product13(e, m):
            slots = slice(e * C, (e + 1) * C)
            w_words, w_scales = codes(m)
            sums[e, m] = bank((2 * e + m) % 4, H)
            nc.tensor.matmul_mx(out=sums[e, m][:], lhsT=slot_words[:, slots].bitcast(FP8X4), lhsT_scale=slot_scales[:, slots],
                                rhs=w_words[:].bitcast(FP8X4), rhs_scale=w_scales[:], start=True, stop=True)

        def activate(e, place):
            acts[e] = place
            nc.scalar.activation(place, sums[e, 0][:], GELU)

        def hidden_rows(e, pairs):
            nc.vector.tensor_tensor(pairs.bitcast(BF16), sums[e, 1][:], acts[e], MULT)
            turned[e] = bank(4 + e % 2, 2 * C)
            for u in range(2):
                nc.tensor.transpose(turned[e][:, u * C : (u + 1) * C], pairs[:, u : H // 2 : 2], ident[:])

        def hidden_codes(e, pairs):
            slots = slice(e * C, (e + 1) * C)
            nc.scalar.copy(pairs.rearrange("p (s u) -> p s u", u=2), turned[e][:].rearrange("p (u s) -> p s u", u=2))
            nc.vector.quantize_mx(out=h_words[:, slots].bitcast(FP8X4), scales=h_scales[:, slots], in_=pairs.bitcast(BF16))

        for a in range(2):
            fetch_tokens(slot_words, tok_words, a)
        for a in range(RUN // 4):
            spread_gate(a)
        for e in range(E):
            cast_whole(0, raw13[e, 0][:], VEC_13.get((e, 0), H))
            if e == 0:
                fetch_tokens(slot_scales, tok_scales, 0)
            if e > 0:
                hidden_rows(e - 1, raw13[e, 0][:, 0, : H // 2])
            product13(e, 0)
            cast_whole(1, raw13[e, 1][:], VEC_13.get((e, 1), 0))
            if e == 0:
                fetch_tokens(slot_scales, tok_scales, 1)
            product13(e, 1)
            if e > 0:
                hidden_codes(e - 1, raw13[e, 1][:, 0, H // 2 :])
            activate(e, raw13[e, 1][:, PACK - 1, :])

        def second(out_cols, words, scales, cols, e):
            slots = slice(e * C, (e + 1) * C)
            nc.tensor.matmul_mx(out=out_cols, lhsT=words[:, cols].bitcast(FP8X4), lhsT_scale=scales[:, cols],
                                rhs=h_words[:, slots].bitcast(FP8X4), rhs_scale=h_scales[:, slots], start=True, stop=True)

        whole_codes = []
        for e in range(WHOLE):
            cast_whole(e, whole2[e][:], VEC_LATE)
            if e == 0:
                hidden_rows(E - 1, whole2[e][:, 0, : H // 2])
            else:
                hidden_codes(E - 1, whole2[e][:, 0, K // 2 :])
            whole_codes.append(codes(e))

        staged = {}
        late = {}

        def shared(b, a, shape, dtype):
            return keep.tile(shape, dtype, name="shared", tag=f"shared{b}_{a}", align_bytes=64)

        def cast2(b, u, copy):
            if u % 2 == 0:
                staged[b, u // 2] = shared(b, u // 2, [P, 2 * PIECE], BF16)
            place = staged[b, u // 2][:, (u % 2) * PIECE : (u % 2 + 1) * PIECE]
            interleave(copy, place.rearrange("p (c j) -> p c j", j=PACK), raw2[b, u].rearrange("p (j n) -> p j n", j=PACK))

        def product2(b, first, count, y):
            a = first // 2
            if first % 2 == 0:
                if a == 0:
                    late[b, a] = (ring2.tile([P, 2 * P], U32, name="late_words", align_bytes=64), ring2.tile([P, 2 * P], U8, name="late_scales", align_bytes=64))
                else:
                    late[b, a] = (shared(b + 1, 0, [P, 2 * P], U32), shared(b + 1, 1, [P, 2 * P], U8))
            words, scales = late[b, a]
            at = first % 2
            cols = slice(at * P, (at + count) * P)
            nc.vector.quantize_mx(out=words[:, cols].bitcast(FP8X4), scales=scales[:, cols], in_=staged[b, a][:, at * PIECE : (at + count) * PIECE])
            for u in range(count):
                second(y[:, u * C : (u + 1) * C], words, scales, slice((at + u) * P, (at + u + 1) * P), WHOLE + first + u)

        def first_four(b):
            y = bank(b % 2, 4 * C)
            for e in range(WHOLE):
                second(y[:, e * C : (e + 1) * C], *whole_codes[e], slice(b * P, (b + 1) * P), e)
            product2(b, 0, 2, y[:, WHOLE * C :])
            nc.scalar.copy(window[b][:, : 4 * C], y[:])

        def last_two(b):
            if b < LAST:
                for u in (2, 3):
                    y = bank(u, C)
                    product2(b, u, 1, y)
                    copy = nc.vector.tensor_copy if (b, u) == (0, 3) else nc.scalar.copy
                    copy(window[b][:, (WHOLE + u) * C : (WHOLE + u + 1) * C], y[:])
            else:
                y = bank(2 + b % 2, 2 * C)
                product2(b, 2, 2, y)
                nc.scalar.copy(window[b][:, 4 * C : SLOTS], y[:])

        picked = {}
        summed = {}
        one_bank = {}
        summed_sb = {}

        def fetch(b, r, cols=slice(0, T)):
            offsets = pos_sb[r][:, cols.start // 16 : cols.stop // 16]
            nc.vector.tensor_tensor(picked[b, r][:, cols], window[b][:].indirect(offsets), gates[:, r, cols], MULT)

        def add_pass(b, c, r):
            nc.tensor.matmul(summed[b][c], lhsT=picked[b, r][:, c * P : (c + 1) * P], rhs=ident[:], is_transpose=True, start=r == 0, stop=r == TOP - 1)

        def add_in_one_bank(b, i):
            whole = bank(i, T)
            summed[b] = [whole[:, c * P : (c + 1) * P] for c in range(T // P)]
            one_bank[b] = whole[:]
            for c in range(T // P):
                for r in range(TOP):
                    add_pass(b, c, r)

        def add_in_banks(b, banks):
            summed[b] = [bank(i, P)[:] for i in banks]
            for r in range(TOP):
                for c in range(len(banks)):
                    add_pass(b, c, r)

        def empty_turned(b, place):
            summed_sb[b] = place
            if b in one_bank:
                nc.scalar.copy(place, one_bank[b])
            else:
                for c in range(len(summed[b])):
                    nc.scalar.copy(place[:, c * P : (c + 1) * P], summed[b][c])

        def turn_back(b, i, total):
            width = len(summed[b]) * P
            back = bank(i, width)
            for c in range(len(summed[b])):
                nc.tensor.transpose(back[:, c * P : (c + 1) * P], summed_sb[b][:, c * P : (c + 1) * P], ident[:])
            nc.scalar.copy(total, back[:])
            (nc.scalar if b >= LAST - 1 else nc.sync).dma_start(out[b * P : (b + 1) * P, :width], total)

        left, right = slice(0, T // 2), slice(T // 2, T)
        for u in range(CUT):
            cast2(0, u, nc.vector.tensor_copy if u == CUT - 1 else nc.scalar.copy)
            if u == 1:
                first_four(0)
        last_two(0)
        for b in range(LAST):
            picked[b, 0] = ring2.tile([P, T], F32, name="picked0")[:]
            fetch(b, 0)
            for u in range(CUT):
                cast2(b + 1, u, nc.scalar.copy)
            first_four(b + 1)
            if b == 1:
                empty_turned(0, wide[2][:, T:])
            if b == 2:
                turn_back(0, 2, wide[LAST][:, T:])
            picked[b, 1] = raw2[b + 1, 1]
            fetch(b, 1)
            last_two(b + 1)
            picked[b, 2] = wide[b + 1][:, :T]
            fetch(b, 2)
            if b < LAST - 1:
                add_in_one_bank(b, 4 + b)
            else:
                add_in_banks(b, (6, 7, 4, 0))
        empty_turned(1, shared(BLOCKS, 0, [P, T], F32)[:])
        empty_turned(2, raw13[2, 0][:, 2, :])
        turn_back(1, 3, raw13[1, 0][:, 1, :])
        for r in range(TOP):
            picked[LAST, r] = raw13[LAST, 1][:, r, :]
        for r in range(TOP):
            fetch(LAST, r, left)
        add_in_banks(LAST, (1, 2))
        empty_turned(LAST, raw13[LAST, 0][:, 3, left])
        turn_back(2, 5, raw13[2, 0][:, 1, :])
        turn_back(LAST, 6, raw13[LAST, 0][:, 1, left])
        for r in range(TOP):
            fetch(LAST, r, right)
        two = raw13[LAST, 0][:, 2, right]
        total = raw13[LAST, 0][:, 1, right]
        nc.vector.tensor_tensor(two, picked[LAST, 0][:, right], picked[LAST, 1][:, right], ADD)
        nc.vector.tensor_tensor(total, two, picked[LAST, 2][:, right], ADD)
        nc.sync.dma_start(out[LAST * P :, right], total)
